import numpy as np
import ml_dtypes


def mxq(x, axis, fmt="e4m3"):
    dtype, down = {"e4m3": (ml_dtypes.float8_e4m3fn, 7), "e5m2": (ml_dtypes.float8_e5m2, 14)}[fmt]
    v = np.moveaxis(np.asarray(x, np.float32).astype(ml_dtypes.bfloat16).astype(np.float64), axis, -1)
    blocks = v.reshape(v.shape[:-1] + (-1, 32))
    amax = np.abs(blocks).max(-1, keepdims=True)
    byte = np.maximum(np.where(amax > 0, np.frexp(amax)[1] - 1 + 127, 0) - down, 1)
    scale = np.exp2(byte - 127.0)
    codes = (blocks / scale).astype(np.float32).astype(dtype).astype(np.float64)
    return np.moveaxis((codes * scale).reshape(v.shape), -1, axis)


WIDE = False


def mx_kscale(k):
    if not WIDE:
        return np.ones(k)
    levels = np.array([10, -10, 5, -5, 0])
    if k % 512:
        return np.exp2(np.random.permutation(np.resize(levels, k // 32))).repeat(32)
    a = np.empty((k // 512, 16))
    for p in range(k // 512):
        a[p, :8] = np.random.permutation(np.resize(levels, 8))
        for g in range(8):
            far = levels[np.abs(levels - a[p, g]) >= 10]
            a[p, g + 8] = far[np.random.randint(len(far))]
    return np.exp2(a.ravel()).repeat(32)


def f64(x):
    return np.asarray(x).astype(np.float64)


def striped(idx):
    return np.tile(idx.reshape(-1, 16).T, (8, 1)).astype(np.uint16)


def unstriped(offs):
    return offs[:16].T.reshape(-1).astype(np.int64)


def relu(v):
    return np.maximum(v, 0.0)


K, T, D, V, H, N = 512, 512, 4, 256, 1024, 256
P = 2 ** 7


def setup_inputs():
    n = np.random.standard_normal
    s = mx_kscale(K)[:, None]
    u = mx_kscale(H)
    return {
        "xT": (n((K, T)) * s).astype(np.float32),
        "w1": (n((K, H)) / np.sqrt(K) / s * u).astype(np.float32),
        "w2": (n((H, N)) / np.sqrt(H) / u[:, None]).astype(np.float32),
        "gate": np.tile(np.random.uniform(0.2, 1.0, (D, 1, V)) / np.sqrt(D), (1, P, 1)).astype(np.float32),
        "pos1": striped(np.random.permutation(T)[:V]),
        "pos2": striped(np.random.permutation(T)[:V]),
        "pos3": striped(np.random.permutation(T)[:V]),
        "pos4": striped(np.random.permutation(T)[:V]),
    }


def reference(xT, w1, w2, gate, pos1, pos2, pos3, pos4):
    h = relu(mxq(f64(w1), 0, "e4m3").T @ mxq(f64(xT), 0, "e4m3"))
    z = sum(f64(gate)[d, :1] * h[:, unstriped(p)] for d, p in enumerate((pos1, pos2, pos3, pos4)))
    return mxq(f64(w2), 0, "e4m3").T @ mxq(z, 0, "e4m3")

@@ -1,0 +1,309 @@
+from contextlib import ExitStack
+
+import concourse.mybir as mybir
+from concourse.masks import make_identity
+
+K, T, D, V, H, N = 512, 512, 4, 256, 1024, 256
+P = 128
+PACK = 4
+BLOCKS = H // P
+HALVES = H // (P * PACK)
+SIDES = V // P
+FLOPS = 2 * K * H * T + 2 * H * N * V
+
+F32 = mybir.dt.float32
+BF16 = mybir.dt.bfloat16
+U32 = mybir.dt.uint32
+U16 = mybir.dt.uint16
+U8 = mybir.dt.uint8
+FP8X4 = mybir.dt.float8_e4m3fn_x4
+MULT = mybir.AluOpType.mult
+RELU = mybir.ActivationFunctionType.Relu
+
+X_PIECES = ((0, 256), (256, 128), (384, 128))
+
+W1_PIECES = ((0, 128), (128, 128), (256, 256), (512, 256), (768, 256))
+
+
+def tile_picked_gcn_mlp_relu_sub_l_kernel(
+    tc, xT, w1, w2, gate, pos1, pos2, pos3, pos4, out
+):
+    nc = tc.nc
+    with ExitStack() as ctx:
+        keep = ctx.enter_context(tc.tile_pool(name="keep", bufs=1))
+        weights = ctx.enter_context(tc.tile_pool(name="weights", bufs=2))
+        raws = ctx.enter_context(tc.tile_pool(name="raws", bufs=3))
+        h_pool = ctx.enter_context(tc.tile_pool(name="h_pool", bufs=4))
+        gathered = ctx.enter_context(tc.tile_pool(name="gathered", bufs=10))
+        psum_h = ctx.enter_context(tc.psum_pool(name="psum_h", bufs=2))
+        psum_sum = ctx.enter_context(tc.psum_pool(name="psum_sum", bufs=2))
+        psum_one = ctx.enter_context(tc.psum_pool(name="psum_one", bufs=1))
+
+
+        def load(pool, name, rows):
+            raw = pool.tile([P, PACK, rows.shape[1]], F32, name=name)
+            nc.sync.dma_start(out=raw[:], in_=rows.rearrange("(p j) w -> p j w", j=PACK))
+            return raw
+
+        def load_w1(pool, name, piece):
+            first, count = W1_PIECES[piece]
+            return load(pool, name, w1[:, first : first + count])
+
+        lists = [keep.tile([P, V // 16], U16, name="list%d" % d) for d in range(D)]
+        gates = keep.tile([P, D, V], F32, name="gates")
+
+        w1_raw = [load_w1(keep, "w1_raw0", 0)]
+        nc.sync.dma_start(lists[0][:], pos1)
+        x_raw = [
+            load(keep, "x_raw%d" % i, xT[:, first : first + count]) for i, (first, count) in enumerate(X_PIECES)
+        ]
+        w1_raw.append(load_w1(keep, "w1_raw1", 1))
+        nc.sync.dma_start(out=gates[:, 0, :], in_=gate[0])
+        nc.sync.dma_start(lists[1][:], pos2)
+        nc.sync.dma_start(out=gates[:, 1:D, :], in_=gate[1:D].rearrange("d p v -> p d v"))
+        nc.sync.dma_start(lists[2][:], pos3)
+        w1_raw.append(load_w1(raws, "w_raw", 2))
+        nc.sync.dma_start(lists[3][:], pos4)
+        w1_raw.append(load_w1(raws, "w_raw", 3))
+        w1_raw.append(load_w1(raws, "w_raw", 4))
+        w2_raw = []
+
+        def load_w2(half):
+            w2_raw.append(load(raws, "w_raw", w2[512 * half : 512 * (half + 1), :]))
+
+        identity = keep.tile([P, P], F32, name="identity")
+        make_identity(nc, identity[:])
+
+
+        def interleave(copy, grouped, raw):
+            copy(
+                out=grouped[:].rearrange("p (c i) j -> p c j i", i=4),
+                in_=raw[:].rearrange("p j (c i) -> p c j i", i=4),
+            )
+
+        def quantise(name, grouped):
+            width = grouped.shape[1]
+            codes = keep.tile([P, width], U32, align_bytes=64, name=name + "_codes")
+            scales = keep.tile([P, width], U8, align_bytes=64, name=name + "_scales")
+            nc.vector.quantize_mx(
+                out=codes[:].bitcast(FP8X4), scales=scales[:], in_=grouped[:].rearrange("p w j -> p (w j)")
+            )
+            return codes, scales
+
+        x_grouped = [
+            keep.tile([P, count, PACK], BF16, align_bytes=64, name="x_grouped%d" % i)
+            for i, (first, count) in enumerate(X_PIECES)
+        ]
+        x_quantised = []
+
+        def copy_x(piece):
+            interleave(nc.vector.tensor_copy, x_grouped[piece], x_raw[piece])
+
+        def quantise_x(piece):
+            x_quantised.append(quantise("x%d" % piece, x_grouped[piece]))
+
+        w1_grouped = []
+        w1_quantised = []
+
+        def copy_w1(piece, copy):
+            count = W1_PIECES[piece][1]
+            if count == P:
+                grouped = keep.tile([P, count, PACK], BF16, align_bytes=64, name="w1_grouped%d" % piece)
+            else:
+                grouped = weights.tile([P, count, PACK], BF16, align_bytes=64, name="w_grouped")
+            interleave(copy, grouped, w1_raw[piece])
+            w1_grouped.append(grouped)
+
+        def quantise_w1(piece):
+            codes, scales = quantise("w1_%d" % piece, w1_grouped[piece])
+            for column in range(0, W1_PIECES[piece][1], P):
+                w1_quantised.append((codes, scales, column))
+
+        w2_grouped = []
+        w2_quantised = []
+
+        def copy_w2(half):
+            grouped = weights.tile([P, N, PACK], BF16, align_bytes=64, name="w_grouped")
+            interleave(nc.scalar.copy, grouped, w2_raw[half])
+            w2_grouped.append(grouped)
+
+        def quantise_w2(half):
+            w2_quantised.append(quantise("w2_%d" % half, w2_grouped[half]))
+
+
+        h_tiles = []
+
+        def project(block, piece, result):
+            codes, scales, column = w1_quantised[block]
+            nc.tensor.matmul_mx(
+                out=result,
+                lhsT=codes[:, column : column + P].bitcast(FP8X4),
+                lhsT_scale=scales[:, column : column + P],
+                rhs=x_quantised[piece][0][:].bitcast(FP8X4),
+                rhs_scale=x_quantised[piece][1][:],
+                start=True,
+                stop=True,
+            )
+
+        def first_product_of_block_0():
+            h = h_pool.tile([P, T], F32, name="h")
+            for piece, bank in enumerate(("out0", "turned0", "turned1")):
+                first, count = X_PIECES[piece]
+                result = psum_one.tile([P, count], F32, name=bank)
+                project(0, piece, result[:])
+                if piece == len(X_PIECES) - 1:
+                    nc.vector.tensor_scalar_max(h[:, first : first + count], result[:], 0.0)
+                else:
+                    nc.scalar.activation(out=h[:, first : first + count], in_=result[:], func=RELU)
+            h_tiles.append(h)
+
+        def first_product(block):
+            result = psum_h.tile([P, T], F32, name="result")
+            h = h_pool.tile([P, T], F32, name="h")
+            for piece, (first, count) in enumerate(X_PIECES):
+                project(block, piece, result[:, first : first + count])
+            nc.scalar.activation(out=h[:], in_=result[:], func=RELU)
+            h_tiles.append(h)
+
+
+        summed = [
+            keep.tile([P, SIDES, P * PACK], BF16, align_bytes=64, name="summed%d" % half) for half in range(HALVES)
+        ]
+
+        def gather(block, d, first=0, last=V):
+            g = gathered.tile([P, V], F32, name="g")
+            nc.vector.tensor_tensor(
+                g[:, first:last],
+                h_tiles[block][:].indirect(lists[d][:, first // 16 : last // 16]),
+                gates[:, d, first:last],
+                MULT,
+            )
+            return g
+
+        def add_turned(total, g, side, d):
+            nc.tensor.matmul(
+                total,
+                lhsT=g[:, P * side : P * (side + 1)],
+                rhs=identity[:],
+                start=(d == 0),
+                stop=(d == D - 1),
+                is_transpose=True,
+            )
+
+        def sum_block(block, gs):
+            total = psum_sum.tile([P, SIDES, P], F32, name="total")
+            for side in range(SIDES):
+                for d in range(D):
+                    add_turned(total[:, side, :], gs[d], side, d)
+            half, quarter = divmod(block, PACK)
+            nc.scalar.copy(out=summed[half][:, :, P * quarter : P * (quarter + 1)], in_=total[:])
+
+
+        z_grouped = [
+            keep.tile([P, SIDES, P * PACK], BF16, align_bytes=64, name="z_grouped%d" % half)
+            for half in range(HALVES)
+        ]
+        z_codes = [keep.tile([P, V], U32, align_bytes=64, name="z_codes%d" % half) for half in range(HALVES)]
+        z_scales = [keep.tile([P, V], U8, align_bytes=64, name="z_scales%d" % half) for half in range(HALVES)]
+
+        def turn_back(half, side, copy):
+            words = summed[half][:, side, :].bitcast(F32)
+            turned = psum_one.tile([P, 2, P], F32, name="turned%d" % side)
+            for u in range(2):
+                nc.tensor.transpose(turned[:, u, :], words[:, u::2], identity[:])
+            copy(
+                out=z_grouped[half][:, side, :].bitcast(F32).rearrange("p (v u) -> p v u", u=2),
+                in_=turned[:].rearrange("p u v -> p v u"),
+            )
+
+        def quantise_z(half, first_side, last_side):
+            columns = slice(P * first_side, P * last_side)
+            nc.vector.quantize_mx(
+                out=z_codes[half][:, columns].bitcast(FP8X4),
+                scales=z_scales[half][:, columns],
+                in_=z_grouped[half][:, first_side:last_side, :].rearrange("p s w -> p (s w)"),
+            )
+
+        out_banks = []
+
+        def second_product(half):
+            for rows in range(N // P):
+                if half == 0:
+                    out_banks.append(psum_one.tile([P, V], F32, name="out%d" % rows))
+                columns = slice(P * rows, P * (rows + 1))
+                nc.tensor.matmul_mx(
+                    out=out_banks[rows][:],
+                    lhsT=w2_quantised[half][0][:, columns].bitcast(FP8X4),
+                    lhsT_scale=w2_quantised[half][1][:, columns],
+                    rhs=z_codes[half][:].bitcast(FP8X4),
+                    rhs_scale=z_scales[half][:],
+                    start=(half == 0),
+                    stop=(half == HALVES - 1),
+                )
+
+
+        scalar_copy = nc.scalar.copy
+        steps = {
+            (1, 0): [
+                (quantise_w1, 2),
+                (first_product, 2),
+                (first_product, 3),
+                (copy_w1, 3, scalar_copy),
+                (load_w2, 0),
+            ],
+            (2, 2): [(quantise_w1, 3), (first_product, 4), (first_product, 5)],
+            (3, 0): [(copy_w1, 4, scalar_copy), (load_w2, 1)],
+            (4, 1): [(quantise_w1, 4), (first_product, 6), (first_product, 7)],
+            (4, 2): [(turn_back, 0, 0, scalar_copy), (turn_back, 0, 1, scalar_copy), (copy_w2, 0)],
+            (5, 1): [(copy_w2, 1)],
+            (5, 2): [(quantise_w2, 0)],
+            (6, 0): [(quantise_z, 0, 0, SIDES)],
+            (6, 1): [(second_product, 0)],
+            (6, 3): [(quantise_w2, 1)],
+        }
+
+        copy_w1(0, scalar_copy)
+        copy_x(0)
+        quantise_w1(0)
+        quantise_x(0)
+        copy_x(1)
+        copy_x(2)
+        quantise_x(1)
+        quantise_x(2)
+        first_product_of_block_0()
+        copy_w1(1, nc.vector.tensor_copy)
+        quantise_w1(1)
+        first_product(1)
+        copy_w1(2, scalar_copy)
+
+        for block in range(BLOCKS - 1):
+            gs = []
+            for d in range(D):
+                gs.append(gather(block, d))
+                for step in steps.get((block, d), []):
+                    step[0](*step[1:])
+            sum_block(block, gs)
+
+        last = BLOCKS - 1
+        copies = (nc.scalar.copy, nc.vector.tensor_copy)
+        gs = [gather(last, d) for d in range(2)]
+        totals = []
+        for side in range(SIDES):
+            total = psum_one.tile([P, P], F32, name="turned%d" % side)
+            totals.append(total)
+            for d in range(2):
+                add_turned(total[:], gs[d], side, d)
+        for side in range(SIDES):
+            for d in range(2, D):
+                g = gather(last, d, P * side, P * (side + 1))
+                add_turned(totals[side][:], g, side, d)
+            copies[side](out=summed[1][:, side, P * (PACK - 1) : P * PACK], in_=totals[side][:])
+            turn_back(1, side, copies[side])
+        for side in range(SIDES):
+            quantise_z(1, side, side + 1)
+        second_product(1)
+
+        for rows, (copy, queue) in enumerate(((nc.vector.tensor_copy, nc.sync), (nc.scalar.copy, nc.scalar))):
+            result = keep.tile([P, V], F32, name="stored%d" % rows)
+            copy(out=result[:], in_=out_banks[rows][:])
+            queue.dma_start(out=out[P * rows : P * (rows + 1), :], in_=result[:])

@@ -22,7 +22,7 @@ RELU = mybir.ActivationFunctionType.Relu
 
 X_PIECES = ((0, 256), (256, 128), (384, 128))
 
-W1_PIECES = ((0, 128), (128, 128), (256, 256), (512, 256), (768, 256))
+W1_PIECES = ((0, 128), (128, 128), (256, 128), (384, 128), (512, 256), (768, 256))
 
 
 def tile_picked_gcn_mlp_relu_sub_l_kernel(
@@ -31,45 +31,43 @@ def tile_picked_gcn_mlp_relu_sub_l_kernel(
     nc = tc.nc
     with ExitStack() as ctx:
         keep = ctx.enter_context(tc.tile_pool(name="keep", bufs=1))
-        weights = ctx.enter_context(tc.tile_pool(name="weights", bufs=2))
-        raws = ctx.enter_context(tc.tile_pool(name="raws", bufs=3))
-        h_pool = ctx.enter_context(tc.tile_pool(name="h_pool", bufs=4))
-        gathered = ctx.enter_context(tc.tile_pool(name="gathered", bufs=10))
-        psum_h = ctx.enter_context(tc.psum_pool(name="psum_h", bufs=2))
-        psum_sum = ctx.enter_context(tc.psum_pool(name="psum_sum", bufs=2))
+        h_pool = ctx.enter_context(tc.tile_pool(name="h_pool", bufs=8))
         psum_one = ctx.enter_context(tc.psum_pool(name="psum_one", bufs=1))
 
 
-        def load(pool, name, rows):
-            raw = pool.tile([P, PACK, rows.shape[1]], F32, name=name)
+        def load(name, rows):
+            raw = keep.tile([P, PACK, rows.shape[1]], F32, name=name)
             nc.sync.dma_start(out=raw[:], in_=rows.rearrange("(p j) w -> p j w", j=PACK))
             return raw
 
-        def load_w1(pool, name, piece):
+        def load_w1(piece):
             first, count = W1_PIECES[piece]
-            return load(pool, name, w1[:, first : first + count])
+            return load("w1_raw%d" % piece, w1[:, first : first + count])
 
         lists = [keep.tile([P, V // 16], U16, name="list%d" % d) for d in range(D)]
-        gates = keep.tile([P, D, V], F32, name="gates")
+        gate01 = keep.tile([P, 2, V], F32, align_bytes=64, name="gate01")
+        gate23 = keep.tile([P, 2, V], F32, name="gate23")
+        gates = [gate01[:, 0, :], gate01[:, 1, :], gate23[:, 0, :], gate23[:, 1, :]]
 
-        w1_raw = [load_w1(keep, "w1_raw0", 0)]
+        def load_x(piece):
+            first, count = X_PIECES[piece]
+            return load("x_raw%d" % piece, xT[:, first : first + count])
+
+        x_raw = [load_x(0)]
+        w1_raw = [load_w1(0)]
         nc.sync.dma_start(lists[0][:], pos1)
-        x_raw = [
-            load(keep, "x_raw%d" % i, xT[:, first : first + count]) for i, (first, count) in enumerate(X_PIECES)
-        ]
-        w1_raw.append(load_w1(keep, "w1_raw1", 1))
-        nc.sync.dma_start(out=gates[:, 0, :], in_=gate[0])
         nc.sync.dma_start(lists[1][:], pos2)
-        nc.sync.dma_start(out=gates[:, 1:D, :], in_=gate[1:D].rearrange("d p v -> p d v"))
         nc.sync.dma_start(lists[2][:], pos3)
-        w1_raw.append(load_w1(raws, "w_raw", 2))
         nc.sync.dma_start(lists[3][:], pos4)
-        w1_raw.append(load_w1(raws, "w_raw", 3))
-        w1_raw.append(load_w1(raws, "w_raw", 4))
-        w2_raw = []
-
-        def load_w2(half):
-            w2_raw.append(load(raws, "w_raw", w2[512 * half : 512 * (half + 1), :]))
+        x_raw.append(load_x(1))
+        x_raw.append(load_x(2))
+        w1_raw.append(load_w1(1))
+        nc.sync.dma_start(out=gate01[:], in_=gate[0:2].rearrange("d p v -> p d v"))
+        w1_raw.append(load_w1(2))
+        nc.sync.dma_start(out=gate23[:], in_=gate[2:D].rearrange("d p v -> p d v"))
+        for piece in range(3, len(W1_PIECES)):
+            w1_raw.append(load_w1(piece))
+        w2_raw = [load("w2_raw%d" % half, w2[512 * half : 512 * (half + 1), :]) for half in range(HALVES)]
 
         identity = keep.tile([P, P], F32, name="identity")
         make_identity(nc, identity[:])
@@ -77,233 +75,256 @@ def tile_picked_gcn_mlp_relu_sub_l_kernel(
 
         def interleave(copy, grouped, raw):
             copy(
-                out=grouped[:].rearrange("p (c i) j -> p c j i", i=4),
-                in_=raw[:].rearrange("p j (c i) -> p c j i", i=4),
+                out=grouped.rearrange("p (c i) j -> p c j i", i=4),
+                in_=raw.rearrange("p j (c i) -> p c j i", i=4),
             )
 
-        def quantise(name, grouped):
-            width = grouped.shape[1]
-            codes = keep.tile([P, width], U32, align_bytes=64, name=name + "_codes")
+        def quantise(codes, scales, grouped):
+            nc.vector.quantize_mx(out=codes.bitcast(FP8X4), scales=scales, in_=grouped)
+
+        def operand(name, width, codes_name=None):
+            codes = keep.tile([P, width], U32, align_bytes=64, name=codes_name or name + "_codes")
             scales = keep.tile([P, width], U8, align_bytes=64, name=name + "_scales")
-            nc.vector.quantize_mx(
-                out=codes[:].bitcast(FP8X4), scales=scales[:], in_=grouped[:].rearrange("p w j -> p (w j)")
-            )
             return codes, scales
 
         x_grouped = [
             keep.tile([P, count, PACK], BF16, align_bytes=64, name="x_grouped%d" % i)
             for i, (first, count) in enumerate(X_PIECES)
         ]
-        x_quantised = []
+        x_codes, x_scales = operand("x", T)
 
-        def copy_x(piece):
-            interleave(nc.vector.tensor_copy, x_grouped[piece], x_raw[piece])
+        def copy_x(piece, copy):
+            interleave(copy, x_grouped[piece][:], x_raw[piece][:])
 
         def quantise_x(piece):
-            x_quantised.append(quantise("x%d" % piece, x_grouped[piece]))
+            first, count = X_PIECES[piece]
+            quantise(
+                x_codes[:, first : first + count],
+                x_scales[:, first : first + count],
+                x_grouped[piece][:].rearrange("p w j -> p (w j)"),
+            )
 
         w1_grouped = []
         w1_quantised = []
 
-        def copy_w1(piece, copy):
+        def copy_w1(piece, copy=nc.scalar.copy):
             count = W1_PIECES[piece][1]
-            if count == P:
-                grouped = keep.tile([P, count, PACK], BF16, align_bytes=64, name="w1_grouped%d" % piece)
-            else:
-                grouped = weights.tile([P, count, PACK], BF16, align_bytes=64, name="w_grouped")
-            interleave(copy, grouped, w1_raw[piece])
+            grouped = keep.tile([P, count, PACK], BF16, align_bytes=64, name="w1_grouped%d" % piece)
+            interleave(copy, grouped[:], w1_raw[piece][:])
             w1_grouped.append(grouped)
 
         def quantise_w1(piece):
-            codes, scales = quantise("w1_%d" % piece, w1_grouped[piece])
-            for column in range(0, W1_PIECES[piece][1], P):
+            count = W1_PIECES[piece][1]
+            codes, scales = operand("w1_%d" % piece, count)
+            quantise(codes[:], scales[:], w1_grouped[piece][:].rearrange("p w j -> p (w j)"))
+            for column in range(0, count, P):
                 w1_quantised.append((codes, scales, column))
 
-        w2_grouped = []
-        w2_quantised = []
+        w2_tiles = []
 
         def copy_w2(half):
-            grouped = weights.tile([P, N, PACK], BF16, align_bytes=64, name="w_grouped")
-            interleave(nc.scalar.copy, grouped, w2_raw[half])
-            w2_grouped.append(grouped)
-
-        def quantise_w2(half):
-            w2_quantised.append(quantise("w2_%d" % half, w2_grouped[half]))
+            if half == 0:
+                w2_tiles.append(keep.tile([P, HALVES * N, PACK], BF16, align_bytes=64, name="w2_grouped"))
+            w2_grouped = w2_tiles[0]
+            interleave(nc.scalar.copy, w2_grouped[:, N * half : N * (half + 1), :], w2_raw[half][:])
 
 
         h_tiles = []
+        zeros = {}
+        for block, name in ((1, "w1_grouped3"), (2, "w1_grouped4"), (3, "w1_grouped5"), (5, "w2_grouped")):
+            zeros[block] = keep.tile([P, 1], F32, align_bytes=64, name=name)
+            nc.gpsimd.memset(zeros[block][:], 0.0)
 
-        def project(block, piece, result):
+        def project(block, first, count, result):
             codes, scales, column = w1_quantised[block]
             nc.tensor.matmul_mx(
                 out=result,
                 lhsT=codes[:, column : column + P].bitcast(FP8X4),
                 lhsT_scale=scales[:, column : column + P],
-                rhs=x_quantised[piece][0][:].bitcast(FP8X4),
-                rhs_scale=x_quantised[piece][1][:],
+                rhs=x_codes[:, first : first + count].bitcast(FP8X4),
+                rhs_scale=x_scales[:, first : first + count],
                 start=True,
                 stop=True,
             )
 
         def first_product_of_block_0():
             h = h_pool.tile([P, T], F32, name="h")
-            for piece, bank in enumerate(("out0", "turned0", "turned1")):
+            zero_v = keep.tile([P, 1], F32, align_bytes=64, name="w1_1_codes")
+            zero_s = keep.tile([P, 1], F32, align_bytes=64, name="w1_grouped1")
+            nc.gpsimd.memset(zero_v[:], 0.0)
+            nc.scalar.activation(out=zero_s[:], in_=zero_v[:], func=RELU)
+            for piece, bank in enumerate(("bank0", "bank1", "bank2")):
                 first, count = X_PIECES[piece]
                 result = psum_one.tile([P, count], F32, name=bank)
-                project(0, piece, result[:])
-                if piece == len(X_PIECES) - 1:
-                    nc.vector.tensor_scalar_max(h[:, first : first + count], result[:], 0.0)
+                project(0, first, count, result[:])
+                if piece > 0:
+                    nc.vector.tensor_scalar_max(h[:, first : first + count], result[:], zero_v[:])
                 else:
-                    nc.scalar.activation(out=h[:, first : first + count], in_=result[:], func=RELU)
+                    nc.scalar.activation(out=h[:, first : first + count], in_=result[:], func=RELU, bias=zero_s[:])
             h_tiles.append(h)
 
         def first_product(block):
-            result = psum_h.tile([P, T], F32, name="result")
             h = h_pool.tile([P, T], F32, name="h")
-            for piece, (first, count) in enumerate(X_PIECES):
-                project(block, piece, result[:, first : first + count])
-            nc.scalar.activation(out=h[:], in_=result[:], func=RELU)
+            if block == 1:
+                for first, bank in ((0, "bank3"), (T // 2, "bank4")):
+                    result = psum_one.tile([P, T // 2], F32, name=bank)
+                    project(block, first, T // 2, result[:])
+                    if first == 0:
+                        nc.scalar.activation(out=h[:, 0 : T // 2], in_=result[:], func=RELU, bias=zeros[block][:])
+                    else:
+                        nc.scalar.activation(out=h[:, T // 2 : T], in_=result[:], func=RELU)
+            else:
+                result = psum_one.tile([P, T], F32, name="bank%d" % ((block + 1) % 3))
+                project(block, 0, T, result[:])
+                if block in zeros:
+                    nc.scalar.activation(out=h[:], in_=result[:], func=RELU, bias=zeros[block][:])
+                else:
+                    nc.scalar.activation(out=h[:], in_=result[:], func=RELU)
             h_tiles.append(h)
 
 
-        summed = [
-            keep.tile([P, SIDES, P * PACK], BF16, align_bytes=64, name="summed%d" % half) for half in range(HALVES)
-        ]
+        summed0 = keep.tile([P, SIDES, 2, P, 2], BF16, align_bytes=64, name="summed0")
+        summed1 = [keep.tile([P, 2, P, 2], BF16, align_bytes=64, name="summed1_%d" % side) for side in range(SIDES)]
+        summed = [[summed0[:, side] for side in range(SIDES)], [summed1[side][:] for side in range(SIDES)]]
 
-        def gather(block, d, first=0, last=V):
-            g = gathered.tile([P, V], F32, name="g")
+        def gather(g, block, d, first=0, last=V):
             nc.vector.tensor_tensor(
-                g[:, first:last],
+                g,
                 h_tiles[block][:].indirect(lists[d][:, first // 16 : last // 16]),
-                gates[:, d, first:last],
+                gates[d][:, first:last],
                 MULT,
             )
-            return g
 
-        def add_turned(total, g, side, d):
-            nc.tensor.matmul(
-                total,
-                lhsT=g[:, P * side : P * (side + 1)],
-                rhs=identity[:],
-                start=(d == 0),
-                stop=(d == D - 1),
-                is_transpose=True,
+        def add_turned(total, g, d):
+            nc.tensor.matmul(total, lhsT=g, rhs=identity[:], start=(d == 0), stop=(d == D - 1), is_transpose=True)
+
+        def leave(block, side, total):
+            half, quarter = divmod(block, PACK)
+            nc.scalar.copy(
+                out=summed[half][side][:, :, 32 * quarter : 32 * (quarter + 1), :],
+                in_=total.rearrange("v (p u e) -> v u p e", u=2, e=2),
             )
 
         def sum_block(block, gs):
-            total = psum_sum.tile([P, SIDES, P], F32, name="total")
+            total = psum_one.tile([P, SIDES, P], F32, name="bank%d" % (5 + block % 3))
             for side in range(SIDES):
                 for d in range(D):
-                    add_turned(total[:, side, :], gs[d], side, d)
-            half, quarter = divmod(block, PACK)
-            nc.scalar.copy(out=summed[half][:, :, P * quarter : P * (quarter + 1)], in_=total[:])
+                    add_turned(total[:, side, :], gs[d][:, P * side : P * (side + 1)], d)
+            if block < PACK:
+                nc.scalar.copy(
+                    out=summed0[:, :, :, 32 * block : 32 * (block + 1), :],
+                    in_=total[:].rearrange("v s (p u e) -> v s u p e", u=2, e=2),
+                )
+            else:
+                for side in range(SIDES):
+                    leave(block, side, total[:, side, :])
 
 
-        z_grouped = [
-            keep.tile([P, SIDES, P * PACK], BF16, align_bytes=64, name="z_grouped%d" % half)
-            for half in range(HALVES)
+        z0_grouped = keep.tile([P, SIDES, P * PACK], BF16, align_bytes=64, name="z0_grouped")
+        z1_grouped = [
+            keep.tile([P, P * PACK], BF16, align_bytes=64, name="z1_grouped%d" % side) for side in range(SIDES)
         ]
-        z_codes = [keep.tile([P, V], U32, align_bytes=64, name="z_codes%d" % half) for half in range(HALVES)]
-        z_scales = [keep.tile([P, V], U8, align_bytes=64, name="z_scales%d" % half) for half in range(HALVES)]
+        z_grouped = [[z0_grouped[:, side, :] for side in range(SIDES)], [z1_grouped[side][:] for side in range(SIDES)]]
 
-        def turn_back(half, side, copy):
-            words = summed[half][:, side, :].bitcast(F32)
-            turned = psum_one.tile([P, 2, P], F32, name="turned%d" % side)
+        def turn_back(half, side):
+            words = summed[half][side].rearrange("v u p e -> v (u p e)").bitcast(F32)
+            turned = psum_one.tile([P, 2, P], F32, name="bank%d" % (3 + side))
             for u in range(2):
-                nc.tensor.transpose(turned[:, u, :], words[:, u::2], identity[:])
-            copy(
-                out=z_grouped[half][:, side, :].bitcast(F32).rearrange("p (v u) -> p v u", u=2),
+                nc.tensor.transpose(turned[:, u, :], words[:, P * u : P * (u + 1)], identity[:])
+            nc.scalar.copy(
+                out=z_grouped[half][side].bitcast(F32).rearrange("p (v u) -> p v u", u=2),
                 in_=turned[:].rearrange("p u v -> p v u"),
             )
 
-        def quantise_z(half, first_side, last_side):
-            columns = slice(P * first_side, P * last_side)
-            nc.vector.quantize_mx(
-                out=z_codes[half][:, columns].bitcast(FP8X4),
-                scales=z_scales[half][:, columns],
-                in_=z_grouped[half][:, first_side:last_side, :].rearrange("p s w -> p (s w)"),
-            )
 
-        out_banks = []
-
-        def second_product(half):
-            for rows in range(N // P):
-                if half == 0:
-                    out_banks.append(psum_one.tile([P, V], F32, name="out%d" % rows))
-                columns = slice(P * rows, P * (rows + 1))
-                nc.tensor.matmul_mx(
-                    out=out_banks[rows][:],
-                    lhsT=w2_quantised[half][0][:, columns].bitcast(FP8X4),
-                    lhsT_scale=w2_quantised[half][1][:, columns],
-                    rhs=z_codes[half][:].bitcast(FP8X4),
-                    rhs_scale=z_scales[half][:],
-                    start=(half == 0),
-                    stop=(half == HALVES - 1),
-                )
-
-
-        scalar_copy = nc.scalar.copy
         steps = {
-            (1, 0): [
-                (quantise_w1, 2),
-                (first_product, 2),
-                (first_product, 3),
-                (copy_w1, 3, scalar_copy),
-                (load_w2, 0),
-            ],
-            (2, 2): [(quantise_w1, 3), (first_product, 4), (first_product, 5)],
-            (3, 0): [(copy_w1, 4, scalar_copy), (load_w2, 1)],
-            (4, 1): [(quantise_w1, 4), (first_product, 6), (first_product, 7)],
-            (4, 2): [(turn_back, 0, 0, scalar_copy), (turn_back, 0, 1, scalar_copy), (copy_w2, 0)],
+            (0, 0): [(quantise_w1, 1), (copy_w1, 2), (first_product, 1), (copy_w1, 3)],
+            (0, 2): [(quantise_w1, 2), (first_product, 2), (copy_w1, 4)],
+            (1, 1): [(quantise_w1, 3), (first_product, 3), (copy_w1, 5)],
+            (2, 1): [(quantise_w1, 4), (first_product, 4), (first_product, 5)],
+            (3, 1): [(quantise_w1, 5), (first_product, 6), (first_product, 7)],
+            (4, 2): [(turn_back, 0, 0), (turn_back, 0, 1), (copy_w2, 0)],
             (5, 1): [(copy_w2, 1)],
-            (5, 2): [(quantise_w2, 0)],
-            (6, 0): [(quantise_z, 0, 0, SIDES)],
-            (6, 1): [(second_product, 0)],
-            (6, 3): [(quantise_w2, 1)],
         }
 
-        copy_w1(0, scalar_copy)
-        copy_x(0)
-        quantise_w1(0)
+        copy_x(0, nc.vector.tensor_copy)
+        copy_w1(0, nc.vector.tensor_copy)
         quantise_x(0)
-        copy_x(1)
-        copy_x(2)
+        quantise_w1(0)
+        copy_x(1, nc.vector.tensor_copy)
+        copy_x(2, nc.vector.tensor_copy)
         quantise_x(1)
         quantise_x(2)
         first_product_of_block_0()
-        copy_w1(1, nc.vector.tensor_copy)
-        quantise_w1(1)
-        first_product(1)
-        copy_w1(2, scalar_copy)
+        copy_w1(1)
 
         for block in range(BLOCKS - 1):
             gs = []
             for d in range(D):
-                gs.append(gather(block, d))
+                g = keep.tile([P, V], F32, name="g%d_%d" % (block, d))
+                gather(g[:], block, d)
+                gs.append(g)
                 for step in steps.get((block, d), []):
                     step[0](*step[1:])
             sum_block(block, gs)
 
         last = BLOCKS - 1
-        copies = (nc.scalar.copy, nc.vector.tensor_copy)
-        gs = [gather(last, d) for d in range(2)]
+        gs = [keep.tile([P, V], F32, align_bytes=64, name="last_g%d" % d) for d in range(2)]
+        for d in range(2):
+            gather(gs[d][:], last, d)
         totals = []
         for side in range(SIDES):
-            total = psum_one.tile([P, P], F32, name="turned%d" % side)
+            total = psum_one.tile([P, P], F32, name="bank%d" % (3 + side))
             totals.append(total)
             for d in range(2):
-                add_turned(total[:], gs[d], side, d)
+                add_turned(total[:], gs[d][:, P * side : P * (side + 1)], d)
         for side in range(SIDES):
             for d in range(2, D):
-                g = gather(last, d, P * side, P * (side + 1))
-                add_turned(totals[side][:], g, side, d)
-            copies[side](out=summed[1][:, side, P * (PACK - 1) : P * PACK], in_=totals[side][:])
-            turn_back(1, side, copies[side])
+                g = keep.tile([P, P], F32, name="last_g%d_%d" % (d, side))
+                gather(g[:], last, d, P * side, P * (side + 1))
+                add_turned(totals[side][:], g[:], d)
+            leave(last, side, totals[side][:])
         for side in range(SIDES):
-            quantise_z(1, side, side + 1)
-        second_product(1)
+            turn_back(1, side)
 
-        for rows, (copy, queue) in enumerate(((nc.vector.tensor_copy, nc.sync), (nc.scalar.copy, nc.scalar))):
-            result = keep.tile([P, V], F32, name="stored%d" % rows)
-            copy(out=result[:], in_=out_banks[rows][:])
-            queue.dma_start(out=out[P * rows : P * (rows + 1), :], in_=result[:])
+        w2_codes, w2_scales = operand("w2", HALVES * N, "gate01")
+        quantise(w2_codes[:], w2_scales[:], w2_tiles[0][:].rearrange("p w j -> p (w j)"))
+        z0_codes, z0_scales = operand("z0", V, "last_g0")
+        quantise(z0_codes[:], z0_scales[:], z0_grouped[:].rearrange("p s w -> p (s w)"))
+        z1 = [operand("z1_%d" % side, P) for side in range(SIDES)]
+        for side in range(SIDES):
+            quantise(z1[side][0][:], z1[side][1][:], z1_grouped[side][:])
+
+        def second_product(result, half, rows, codes, scales):
+            columns = slice(N * half + P * rows, N * half + P * (rows + 1))
+            nc.tensor.matmul_mx(
+                out=result,
+                lhsT=w2_codes[:, columns].bitcast(FP8X4),
+                lhsT_scale=w2_scales[:, columns],
+                rhs=codes.bitcast(FP8X4),
+                rhs_scale=scales,
+                start=(half == 0),
+                stop=(half == HALVES - 1),
+            )
+
+        banks = [
+            [psum_one.tile([P, P], F32, name="bank%d" % rows) for rows in range(N // P)],
+            [psum_one.tile([P, P], F32, name="bank%d" % (2 + 4 * rows)) for rows in range(N // P)],
+        ]
+        for side in range(SIDES):
+            columns = slice(P * side, P * (side + 1))
+            for rows in range(N // P):
+                second_product(banks[side][rows][:], 0, rows, z0_codes[:, columns], z0_scales[:, columns])
+        for side in range(SIDES):
+            for rows in range(N // P):
+                second_product(banks[side][rows][:], 1, rows, z1[side][0][:], z1[side][1][:])
+
+        copies = (nc.vector.tensor_copy, nc.scalar.copy)
+        stored0 = keep.tile([P, N // P, P], F32, name="stored0")
+        for rows in range(N // P):
+            copies[rows](out=stored0[:, rows, :], in_=banks[0][rows][:])
+        nc.sync.dma_start(out=out[:, 0:P].rearrange("(r p) v -> p r v", p=P), in_=stored0[:])
+        for rows, queue in enumerate((nc.sync, nc.scalar)):
+            result = keep.tile([P, P], F32, name="stored1_%d" % rows)
+            copies[rows](out=result[:], in_=banks[1][rows][:])
+            queue.dma_start(out=out[P * rows : P * (rows + 1), P:V], in_=result[:])

@@ -166,7 +166,7 @@ def tile_picked_gcn_mlp_relu_sub_l_kernel(
         def first_product(block):
             h = h_pool.tile([P, T], F32, name="h")
             if block == 1:
-                for first, bank in ((0, "bank3"), (T // 2, "bank4")):
+                for first, bank in ((0, "bank3"), (T // 2, "bank0")):
                     result = psum_one.tile([P, T // 2], F32, name=bank)
                     project(block, first, T // 2, result[:])
                     if first == 0:
@@ -174,7 +174,7 @@ def tile_picked_gcn_mlp_relu_sub_l_kernel(
                     else:
                         nc.scalar.activation(out=h[:, T // 2 : T], in_=result[:], func=RELU)
             else:
-                result = psum_one.tile([P, T], F32, name="bank%d" % ((block + 1) % 3))
+                result = psum_one.tile([P, T], F32, name="bank%d" % ((block - 1) % 4))
                 project(block, 0, T, result[:])
                 if block in zeros:
                     nc.scalar.activation(out=h[:], in_=result[:], func=RELU, bias=zeros[block][:])
@@ -206,18 +206,14 @@ def tile_picked_gcn_mlp_relu_sub_l_kernel(
             )
 
         def sum_block(block, gs):
-            total = psum_one.tile([P, SIDES, P], F32, name="bank%d" % (5 + block % 3))
-            for side in range(SIDES):
-                for d in range(D):
-                    add_turned(total[:, side, :], gs[d][:, P * side : P * (side + 1)], d)
-            if block < PACK:
-                nc.scalar.copy(
-                    out=summed0[:, :, :, 32 * block : 32 * (block + 1), :],
-                    in_=total[:].rearrange("v s (p u e) -> v s u p e", u=2, e=2),
-                )
-            else:
+            sums = [
+                psum_one.tile([P, P], F32, name="bank%d" % (4 + 2 * (block % 2) + side)) for side in range(SIDES)
+            ]
+            for d in range(D):
                 for side in range(SIDES):
-                    leave(block, side, total[:, side, :])
+                    add_turned(sums[side][:], gs[d][:, P * side : P * (side + 1)], d)
+            for side in range(SIDES):
+                leave(block, side, sums[side][:])
 
 
         z0_grouped = keep.tile([P, SIDES, P * PACK], BF16, align_bytes=64, name="z0_grouped")
@@ -226,9 +222,9 @@ def tile_picked_gcn_mlp_relu_sub_l_kernel(
         ]
         z_grouped = [[z0_grouped[:, side, :] for side in range(SIDES)], [z1_grouped[side][:] for side in range(SIDES)]]
 
-        def turn_back(half, side):
+        def turn_back(half, side, bank):
             words = summed[half][side].rearrange("v u p e -> v (u p e)").bitcast(F32)
-            turned = psum_one.tile([P, 2, P], F32, name="bank%d" % (3 + side))
+            turned = psum_one.tile([P, 2, P], F32, name=bank)
             for u in range(2):
                 nc.tensor.transpose(turned[:, u, :], words[:, P * u : P * (u + 1)], identity[:])
             nc.scalar.copy(
@@ -239,11 +235,11 @@ def tile_picked_gcn_mlp_relu_sub_l_kernel(
 
         steps = {
             (0, 0): [(quantise_w1, 1), (copy_w1, 2), (first_product, 1), (copy_w1, 3)],
-            (0, 2): [(quantise_w1, 2), (first_product, 2), (copy_w1, 4)],
+            (0, 1): [(quantise_w1, 2), (first_product, 2), (copy_w1, 4)],
             (1, 1): [(quantise_w1, 3), (first_product, 3), (copy_w1, 5)],
             (2, 1): [(quantise_w1, 4), (first_product, 4), (first_product, 5)],
             (3, 1): [(quantise_w1, 5), (first_product, 6), (first_product, 7)],
-            (4, 2): [(turn_back, 0, 0), (turn_back, 0, 1), (copy_w2, 0)],
+            (4, 2): [(turn_back, 0, 0, "bank3"), (turn_back, 0, 1, "bank0"), (copy_w2, 0)],
             (5, 1): [(copy_w2, 1)],
         }
 
@@ -274,7 +270,7 @@ def tile_picked_gcn_mlp_relu_sub_l_kernel(
             gather(gs[d][:], last, d)
         totals = []
         for side in range(SIDES):
-            total = psum_one.tile([P, P], F32, name="bank%d" % (3 + side))
+            total = psum_one.tile([P, P], F32, name="bank%d" % (6 + side))
             totals.append(total)
             for d in range(2):
                 add_turned(total[:], gs[d][:, P * side : P * (side + 1)], d)
@@ -284,8 +280,8 @@ def tile_picked_gcn_mlp_relu_sub_l_kernel(
                 gather(g[:], last, d, P * side, P * (side + 1))
                 add_turned(totals[side][:], g[:], d)
             leave(last, side, totals[side][:])
-        for side in range(SIDES):
-            turn_back(1, side)
+        turn_back(1, 0, "bank6")
+        turn_back(1, 1, "bank4")
 
         w2_codes, w2_scales = operand("w2", HALVES * N, "gate01")
         quantise(w2_codes[:], w2_scales[:], w2_tiles[0][:].rearrange("p w j -> p (w j)"))
@@ -295,7 +291,7 @@ def tile_picked_gcn_mlp_relu_sub_l_kernel(
         for side in range(SIDES):
             quantise(z1[side][0][:], z1[side][1][:], z1_grouped[side][:])
 
-        def second_product(result, half, rows, codes, scales):
+        def second_product(result, half, rows, codes, scales, start):
             columns = slice(N * half + P * rows, N * half + P * (rows + 1))
             nc.tensor.matmul_mx(
                 out=result,
@@ -303,21 +299,21 @@ def tile_picked_gcn_mlp_relu_sub_l_kernel(
                 lhsT_scale=w2_scales[:, columns],
                 rhs=codes.bitcast(FP8X4),
                 rhs_scale=scales,
-                start=(half == 0),
-                stop=(half == HALVES - 1),
+                start=start,
+                stop=not start,
             )
 
         banks = [
-            [psum_one.tile([P, P], F32, name="bank%d" % rows) for rows in range(N // P)],
-            [psum_one.tile([P, P], F32, name="bank%d" % (2 + 4 * rows)) for rows in range(N // P)],
+            [psum_one.tile([P, P], F32, name="bank%d" % (1 + rows)) for rows in range(N // P)],
+            [psum_one.tile([P, P], F32, name="bank%d" % (7 - rows)) for rows in range(N // P)],
         ]
-        for side in range(SIDES):
-            columns = slice(P * side, P * (side + 1))
-            for rows in range(N // P):
-                second_product(banks[side][rows][:], 0, rows, z0_codes[:, columns], z0_scales[:, columns])
-        for side in range(SIDES):
-            for rows in range(N // P):
-                second_product(banks[side][rows][:], 1, rows, z1[side][0][:], z1[side][1][:])
+        for rows in range(N // P):
+            second_product(banks[1][rows][:], 0, rows, z0_codes[:, P:V], z0_scales[:, P:V], True)
+        for rows in range(N // P):
+            second_product(banks[0][rows][:], 1, rows, z1[0][0][:], z1[0][1][:], True)
+            second_product(banks[0][rows][:], 0, rows, z0_codes[:, 0:P], z0_scales[:, 0:P], False)
+        for rows in range(N // P):
+            second_product(banks[1][rows][:], 1, rows, z1[1][0][:], z1[1][1][:], False)
 
         copies = (nc.vector.tensor_copy, nc.scalar.copy)
         stored0 = keep.tile([P, N // P, P], F32, name="stored0")

@@ -55,16 +55,16 @@ def tile_picked_gcn_mlp_relu_sub_l_kernel(
 
         x_raw = [load_x(0)]
         w1_raw = [load_w1(0)]
-        nc.sync.dma_start(lists[0][:], pos1)
-        nc.sync.dma_start(lists[1][:], pos2)
-        nc.sync.dma_start(lists[2][:], pos3)
-        nc.sync.dma_start(lists[3][:], pos4)
         x_raw.append(load_x(1))
         x_raw.append(load_x(2))
         w1_raw.append(load_w1(1))
+        nc.sync.dma_start(lists[0][:], pos1)
         nc.sync.dma_start(out=gate01[:], in_=gate[0:2].rearrange("d p v -> p d v"))
+        nc.sync.dma_start(lists[1][:], pos2)
         w1_raw.append(load_w1(2))
         nc.sync.dma_start(out=gate23[:], in_=gate[2:D].rearrange("d p v -> p d v"))
+        nc.sync.dma_start(lists[2][:], pos3)
+        nc.sync.dma_start(lists[3][:], pos4)
         for piece in range(3, len(W1_PIECES)):
             w1_raw.append(load_w1(piece))
         w2_raw = [load("w2_raw%d" % half, w2[512 * half : 512 * (half + 1), :]) for half in range(HALVES)]
@@ -135,6 +135,11 @@ def tile_picked_gcn_mlp_relu_sub_l_kernel(
             zeros[block] = keep.tile([P, 1], F32, align_bytes=64, name=name)
             nc.gpsimd.memset(zeros[block][:], 0.0)
 
+        zero_first = keep.tile([P, 1], F32, align_bytes=64, name="w1_grouped1")
+        nc.gpsimd.memset(zero_first[:], 0.0)
+        zero_s = keep.tile([P, 1], F32, align_bytes=64, name="w1_grouped2")
+        nc.scalar.activation(out=zero_s[:], in_=identity[:, 0:1], func=RELU, scale=-1.0, bias=zero_first[:])
+
         def project(block, first, count, result):
             codes, scales, column = w1_quantised[block]
             nc.tensor.matmul_mx(
@@ -149,16 +154,12 @@ def tile_picked_gcn_mlp_relu_sub_l_kernel(
 
         def first_product_of_block_0():
             h = h_pool.tile([P, T], F32, name="h")
-            zero_v = keep.tile([P, 1], F32, align_bytes=64, name="w1_1_codes")
-            zero_s = keep.tile([P, 1], F32, align_bytes=64, name="w1_grouped1")
-            nc.gpsimd.memset(zero_v[:], 0.0)
-            nc.scalar.activation(out=zero_s[:], in_=zero_v[:], func=RELU)
             for piece, bank in enumerate(("bank0", "bank1", "bank2")):
                 first, count = X_PIECES[piece]
                 result = psum_one.tile([P, count], F32, name=bank)
                 project(0, first, count, result[:])
                 if piece > 0:
-                    nc.vector.tensor_scalar_max(h[:, first : first + count], result[:], zero_v[:])
+                    nc.vector.tensor_scalar_max(h[:, first : first + count], result[:], zero_s[:])
                 else:
                     nc.scalar.activation(out=h[:, first : first + count], in_=result[:], func=RELU, bias=zero_s[:])
             h_tiles.append(h)
@@ -234,7 +235,7 @@ def tile_picked_gcn_mlp_relu_sub_l_kernel(
 
 
         steps = {
-            (0, 0): [(quantise_w1, 1), (copy_w1, 2), (first_product, 1), (copy_w1, 3)],
+            (0, 0): [(copy_w1, 3)],
             (0, 1): [(quantise_w1, 2), (first_product, 2), (copy_w1, 4)],
             (1, 1): [(quantise_w1, 3), (first_product, 3), (copy_w1, 5)],
             (2, 1): [(quantise_w1, 4), (first_product, 4), (first_product, 5)],
@@ -251,8 +252,11 @@ def tile_picked_gcn_mlp_relu_sub_l_kernel(
         copy_x(2, nc.vector.tensor_copy)
         quantise_x(1)
         quantise_x(2)
-        first_product_of_block_0()
         copy_w1(1)
+        first_product_of_block_0()
+        quantise_w1(1)
+        copy_w1(2)
+        first_product(1)
 
         for block in range(BLOCKS - 1):
             gs = []

@@ -53,10 +53,11 @@ def tile_picked_gcn_mlp_relu_sub_l_kernel(
             first, count = X_PIECES[piece]
             return load("x_raw%d" % piece, xT[:, first : first + count])
 
-        x_raw = [load_x(0)]
+        x_raw = [load_x(0)[:]]
         w1_raw = [load_w1(0)]
-        x_raw.append(load_x(1))
-        x_raw.append(load_x(2))
+        x_rest = load("x_rest", xT[:, T // 2 : T])
+        x_raw.append(x_rest[:, :, 0:P])
+        x_raw.append(x_rest[:, :, P : 2 * P])
         w1_raw.append(load_w1(1))
         nc.sync.dma_start(lists[0][:], pos1)
         nc.sync.dma_start(out=gate01[:], in_=gate[0:2].rearrange("d p v -> p d v"))
@@ -94,7 +95,7 @@ def tile_picked_gcn_mlp_relu_sub_l_kernel(
         x_codes, x_scales = operand("x", T)
 
         def copy_x(piece, copy):
-            interleave(copy, x_grouped[piece][:], x_raw[piece][:])
+            interleave(copy, x_grouped[piece][:], x_raw[piece])
 
         def quantise_x(piece):
             first, count = X_PIECES[piece]
@@ -158,7 +159,7 @@ def tile_picked_gcn_mlp_relu_sub_l_kernel(
                 first, count = X_PIECES[piece]
                 result = psum_one.tile([P, count], F32, name=bank)
                 project(0, first, count, result[:])
-                if piece > 0:
+                if piece < len(X_PIECES) - 1:
                     nc.vector.tensor_scalar_max(h[:, first : first + count], result[:], zero_s[:])
                 else:
                     nc.scalar.activation(out=h[:, first : first + count], in_=result[:], func=RELU, bias=zero_s[:])
@@ -249,7 +250,7 @@ def tile_picked_gcn_mlp_relu_sub_l_kernel(
         quantise_x(0)
         quantise_w1(0)
         copy_x(1, nc.vector.tensor_copy)
-        copy_x(2, nc.vector.tensor_copy)
+        copy_x(2, nc.scalar.copy)
         quantise_x(1)
         quantise_x(2)
         copy_w1(1)
@@ -269,17 +270,18 @@ def tile_picked_gcn_mlp_relu_sub_l_kernel(
             sum_block(block, gs)
 
         last = BLOCKS - 1
-        gs = [keep.tile([P, V], F32, align_bytes=64, name="last_g%d" % d) for d in range(2)]
-        for d in range(2):
+        gs = [keep.tile([P, V], F32, align_bytes=64, name="last_g%d" % d) for d in range(D - 1)]
+        for d in range(D - 1):
             gather(gs[d][:], last, d)
         totals = []
         for side in range(SIDES):
             total = psum_one.tile([P, P], F32, name="bank%d" % (6 + side))
             totals.append(total)
-            for d in range(2):
-                add_turned(total[:], gs[d][:, P * side : P * (side + 1)], d)
+        for d in range(D - 1):
+            for side in range(SIDES):
+                add_turned(totals[side][:], gs[d][:, P * side : P * (side + 1)], d)
         for side in range(SIDES):
-            for d in range(2, D):
+            for d in range(D - 1, D):
                 g = keep.tile([P, P], F32, name="last_g%d_%d" % (d, side))
                 gather(g[:], last, d, P * side, P * (side + 1))
                 add_turned(totals[side][:], g[:], d)

@@ -153,17 +153,17 @@ def tile_picked_gcn_mlp_relu_sub_l_kernel(
                 stop=True,
             )
 
-        def first_product_of_block_0():
-            h = h_pool.tile([P, T], F32, name="h")
-            for piece, bank in enumerate(("bank0", "bank1", "bank2")):
-                first, count = X_PIECES[piece]
-                result = psum_one.tile([P, count], F32, name=bank)
-                project(0, first, count, result[:])
-                if piece < len(X_PIECES) - 1:
-                    nc.vector.tensor_scalar_max(h[:, first : first + count], result[:], zero_s[:])
-                else:
-                    nc.scalar.activation(out=h[:, first : first + count], in_=result[:], func=RELU, bias=zero_s[:])
-            h_tiles.append(h)
+        def first_product_of_block_0(piece):
+            if piece == 0:
+                h_tiles.append(h_pool.tile([P, T], F32, name="h"))
+            h = h_tiles[0]
+            first, count = X_PIECES[piece]
+            result = psum_one.tile([P, count], F32, name="bank%d" % piece)
+            project(0, first, count, result[:])
+            if piece == 1:
+                nc.vector.tensor_scalar_max(h[:, first : first + count], result[:], zero_s[:])
+            else:
+                nc.scalar.activation(out=h[:, first : first + count], in_=result[:], func=RELU, bias=zero_s[:])
 
         def first_product(block):
             h = h_pool.tile([P, T], F32, name="h")
@@ -250,11 +250,14 @@ def tile_picked_gcn_mlp_relu_sub_l_kernel(
         quantise_x(0)
         quantise_w1(0)
         copy_x(1, nc.vector.tensor_copy)
-        copy_x(2, nc.scalar.copy)
+        interleave(nc.vector.tensor_copy, x_grouped[2][:, 0:64, :], x_raw[2][:, :, 0:64])
+        interleave(nc.scalar.copy, x_grouped[2][:, 64:P, :], x_raw[2][:, :, 64:P])
         quantise_x(1)
         quantise_x(2)
-        copy_w1(1)
-        first_product_of_block_0()
+        first_product_of_block_0(0)
+        copy_w1(1, nc.vector.tensor_copy)
+        first_product_of_block_0(1)
+        first_product_of_block_0(2)
         quantise_w1(1)
         copy_w1(2)
         first_product(1)
@@ -282,23 +285,30 @@ def tile_picked_gcn_mlp_relu_sub_l_kernel(
                 add_turned(totals[side][:], gs[d][:, P * side : P * (side + 1)], d)
         for side in range(SIDES):
             for d in range(D - 1, D):
-                g = keep.tile([P, P], F32, name="last_g%d_%d" % (d, side))
+                g = keep.tile([P, P], F32, align_bytes=64, name="last_g%d_%d" % (d, side))
                 gather(g[:], last, d, P * side, P * (side + 1))
                 add_turned(totals[side][:], g[:], d)
             leave(last, side, totals[side][:])
         turn_back(1, 0, "bank6")
         turn_back(1, 1, "bank4")
 
-        w2_codes, w2_scales = operand("w2", HALVES * N, "gate01")
-        quantise(w2_codes[:], w2_scales[:], w2_tiles[0][:].rearrange("p w j -> p (w j)"))
+        w2_quantised = [operand("w2_0", N, "last_g3_1"), operand("w2_1", N, "gate01")]
+
+        def quantise_w2(half):
+            grouped = w2_tiles[0][:, N * half : N * (half + 1), :].rearrange("p w j -> p (w j)")
+            quantise(w2_quantised[half][0][:], w2_quantised[half][1][:], grouped)
+
+        quantise_w2(1)
         z0_codes, z0_scales = operand("z0", V, "last_g0")
         quantise(z0_codes[:], z0_scales[:], z0_grouped[:].rearrange("p s w -> p (s w)"))
+        quantise_w2(0)
         z1 = [operand("z1_%d" % side, P) for side in range(SIDES)]
         for side in range(SIDES):
             quantise(z1[side][0][:], z1[side][1][:], z1_grouped[side][:])
 
         def second_product(result, half, rows, codes, scales, start):
-            columns = slice(N * half + P * rows, N * half + P * (rows + 1))
+            columns = slice(P * rows, P * (rows + 1))
+            w2_codes, w2_scales = w2_quantised[half]
             nc.tensor.matmul_mx(
                 out=result,
                 lhsT=w2_codes[:, columns].bitcast(FP8X4),
@@ -311,15 +321,15 @@ def tile_picked_gcn_mlp_relu_sub_l_kernel(
 
         banks = [
             [psum_one.tile([P, P], F32, name="bank%d" % (1 + rows)) for rows in range(N // P)],
-            [psum_one.tile([P, P], F32, name="bank%d" % (7 - rows)) for rows in range(N // P)],
+            [psum_one.tile([P, P], F32, name="bank%d" % (3 + 2 * rows)) for rows in range(N // P)],
         ]
-        for rows in range(N // P):
-            second_product(banks[1][rows][:], 0, rows, z0_codes[:, P:V], z0_scales[:, P:V], True)
-        for rows in range(N // P):
-            second_product(banks[0][rows][:], 1, rows, z1[0][0][:], z1[0][1][:], True)
-            second_product(banks[0][rows][:], 0, rows, z0_codes[:, 0:P], z0_scales[:, 0:P], False)
-        for rows in range(N // P):
-            second_product(banks[1][rows][:], 1, rows, z1[1][0][:], z1[1][1][:], False)
+        for side in range(SIDES):
+            targets = slice(P * side, P * (side + 1))
+            for rows in range(N // P):
+                second_product(banks[side][rows][:], 0, rows, z0_codes[:, targets], z0_scales[:, targets], True)
+        for side in range(SIDES):
+            for rows in range(N // P):
+                second_product(banks[side][rows][:], 1, rows, z1[side][0][:], z1[side][1][:], False)
 
         copies = (nc.vector.tensor_copy, nc.scalar.copy)
         stored0 = keep.tile([P, N // P, P], F32, name="stored0")

@@ -111,7 +111,13 @@ def tile_picked_gcn_mlp_relu_sub_l_kernel(
         def copy_w1(piece, copy=nc.scalar.copy):
             count = W1_PIECES[piece][1]
             grouped = keep.tile([P, count, PACK], BF16, align_bytes=64, name="w1_grouped%d" % piece)
-            interleave(copy, grouped[:], w1_raw[piece][:])
+            if count == P:
+                interleave(copy, grouped[:], w1_raw[piece][:])
+            else:
+                copy(
+                    out=grouped[:].rearrange("p (u c e) j -> p c j u e", u=2, e=2),
+                    in_=w1_raw[piece][:].rearrange("p j (c u e) -> p c j u e", u=2, e=2),
+                )
             w1_grouped.append(grouped)
 
         def quantise_w1(piece):
@@ -202,10 +208,17 @@ def tile_picked_gcn_mlp_relu_sub_l_kernel(
 
         def leave(block, side, total):
             half, quarter = divmod(block, PACK)
-            nc.scalar.copy(
-                out=summed[half][side][:, :, 32 * quarter : 32 * (quarter + 1), :],
-                in_=total.rearrange("v (p u e) -> v u p e", u=2, e=2),
-            )
+            if half == 0:
+                nc.scalar.copy(
+                    out=summed[half][side][:, :, 32 * quarter : 32 * (quarter + 1), :],
+                    in_=total.rearrange("v (p u e) -> v u p e", u=2, e=2),
+                )
+            else:
+                piece, u = divmod(quarter, 2)
+                nc.scalar.copy(
+                    out=summed[half][side][:, u, 64 * piece : 64 * (piece + 1), :],
+                    in_=total.rearrange("v (p e) -> v p e", e=2),
+                )
 
         def sum_block(block, gs):
             sums = [
@@ -224,11 +237,17 @@ def tile_picked_gcn_mlp_relu_sub_l_kernel(
         ]
         z_grouped = [[z0_grouped[:, side, :] for side in range(SIDES)], [z1_grouped[side][:] for side in range(SIDES)]]
 
+        def turn(turned, half, side, u):
+            words = summed[half][side][:, u].rearrange("v p e -> v (p e)").bitcast(F32)
+            nc.tensor.transpose(turned[:, u, :], words, identity[:])
+
         def turn_back(half, side, bank):
-            words = summed[half][side].rearrange("v u p e -> v (u p e)").bitcast(F32)
             turned = psum_one.tile([P, 2, P], F32, name=bank)
             for u in range(2):
-                nc.tensor.transpose(turned[:, u, :], words[:, P * u : P * (u + 1)], identity[:])
+                turn(turned, half, side, u)
+            weave(turned, half, side)
+
+        def weave(turned, half, side):
             nc.scalar.copy(
                 out=z_grouped[half][side].bitcast(F32).rearrange("p (v u) -> p v u", u=2),
                 in_=turned[:].rearrange("p u v -> p v u"),
@@ -272,25 +291,29 @@ def tile_picked_gcn_mlp_relu_sub_l_kernel(
                     step[0](*step[1:])
             sum_block(block, gs)
 
+        turned1 = [psum_one.tile([P, 2, P], F32, name=bank) for bank in ("bank0", "bank4")]
+        for side in range(SIDES):
+            turn(turned1[side], 1, side, 0)
         last = BLOCKS - 1
-        gs = [keep.tile([P, V], F32, align_bytes=64, name="last_g%d" % d) for d in range(D - 1)]
-        for d in range(D - 1):
+        gs = [keep.tile([P, V], F32, align_bytes=64, name="last_g%d" % d) for d in range(1)]
+        for d in range(1):
             gather(gs[d][:], last, d)
         totals = []
         for side in range(SIDES):
             total = psum_one.tile([P, P], F32, name="bank%d" % (6 + side))
             totals.append(total)
-        for d in range(D - 1):
+        for d in range(1):
             for side in range(SIDES):
                 add_turned(totals[side][:], gs[d][:, P * side : P * (side + 1)], d)
         for side in range(SIDES):
-            for d in range(D - 1, D):
+            for d in range(1, D):
                 g = keep.tile([P, P], F32, align_bytes=64, name="last_g%d_%d" % (d, side))
                 gather(g[:], last, d, P * side, P * (side + 1))
                 add_turned(totals[side][:], g[:], d)
             leave(last, side, totals[side][:])
-        turn_back(1, 0, "bank6")
-        turn_back(1, 1, "bank4")
+        for side in range(SIDES):
+            turn(turned1[side], 1, side, 1)
+            weave(turned1[side], 1, side)
 
         w2_quantised = [operand("w2_0", N, "last_g3_1"), operand("w2_1", N, "gate01")]
 

@@ -22,7 +22,11 @@ RELU = mybir.ActivationFunctionType.Relu
 
 X_PIECES = ((0, 256), (256, 128), (384, 128))
 
+X_VECTOR_SHARE = 64
+
 W1_PIECES = ((0, 128), (128, 128), (256, 128), (384, 128), (512, 256), (768, 256))
+
+WHOLE_NEIGHBOURS = 2
 
 
 def tile_picked_gcn_mlp_relu_sub_l_kernel(
@@ -31,7 +35,7 @@ def tile_picked_gcn_mlp_relu_sub_l_kernel(
     nc = tc.nc
     with ExitStack() as ctx:
         keep = ctx.enter_context(tc.tile_pool(name="keep", bufs=1))
-        h_pool = ctx.enter_context(tc.tile_pool(name="h_pool", bufs=8))
+        h_pool = ctx.enter_context(tc.tile_pool(name="h_pool", bufs=BLOCKS))
         psum_one = ctx.enter_context(tc.psum_pool(name="psum_one", bufs=1))
 
 
@@ -49,26 +53,24 @@ def tile_picked_gcn_mlp_relu_sub_l_kernel(
         gate23 = keep.tile([P, 2, V], F32, name="gate23")
         gates = [gate01[:, 0, :], gate01[:, 1, :], gate23[:, 0, :], gate23[:, 1, :]]
 
-        def load_x(piece):
-            first, count = X_PIECES[piece]
-            return load("x_raw%d" % piece, xT[:, first : first + count])
-
-        x_raw = [load_x(0)[:]]
+        x_raw = [load("x_raw0", xT[:, 0 : T // 2])[:]]
         w1_raw = [load_w1(0)]
         x_rest = load("x_rest", xT[:, T // 2 : T])
         x_raw.append(x_rest[:, :, 0:P])
         x_raw.append(x_rest[:, :, P : 2 * P])
         w1_raw.append(load_w1(1))
         nc.sync.dma_start(lists[0][:], pos1)
-        nc.sync.dma_start(out=gate01[:], in_=gate[0:2].rearrange("d p v -> p d v"))
-        nc.sync.dma_start(lists[1][:], pos2)
+        nc.sync.dma_start(out=gate01[:, 0, :], in_=gate[0])
         w1_raw.append(load_w1(2))
-        nc.sync.dma_start(out=gate23[:], in_=gate[2:D].rearrange("d p v -> p d v"))
+        nc.sync.dma_start(lists[1][:], pos2)
+        nc.sync.dma_start(out=gate01[:, 1, :], in_=gate[1])
+        nc.sync.dma_start(out=gate23[:, 0, :], in_=gate[2])
         nc.sync.dma_start(lists[2][:], pos3)
+        nc.sync.dma_start(out=gate23[:, 1, :], in_=gate[3])
         nc.sync.dma_start(lists[3][:], pos4)
         for piece in range(3, len(W1_PIECES)):
             w1_raw.append(load_w1(piece))
-        w2_raw = [load("w2_raw%d" % half, w2[512 * half : 512 * (half + 1), :]) for half in range(HALVES)]
+        w2_raw = [load("w2_raw%d" % half, w2[P * PACK * half : P * PACK * (half + 1), :]) for half in range(HALVES)]
 
         identity = keep.tile([P, P], F32, name="identity")
         make_identity(nc, identity[:])
@@ -144,8 +146,8 @@ def tile_picked_gcn_mlp_relu_sub_l_kernel(
 
         zero_first = keep.tile([P, 1], F32, align_bytes=64, name="w1_grouped1")
         nc.gpsimd.memset(zero_first[:], 0.0)
-        zero_s = keep.tile([P, 1], F32, align_bytes=64, name="w1_grouped2")
-        nc.scalar.activation(out=zero_s[:], in_=identity[:, 0:1], func=RELU, scale=-1.0, bias=zero_first[:])
+        zero_block_0 = keep.tile([P, 1], F32, align_bytes=64, name="w1_grouped2")
+        nc.scalar.activation(out=zero_block_0[:], in_=identity[:, 0:1], func=RELU, scale=-1.0, bias=zero_first[:])
 
         def project(block, first, count, result):
             codes, scales, column = w1_quantised[block]
@@ -167,9 +169,9 @@ def tile_picked_gcn_mlp_relu_sub_l_kernel(
             result = psum_one.tile([P, count], F32, name="bank%d" % piece)
             project(0, first, count, result[:])
             if piece == 1:
-                nc.vector.tensor_scalar_max(h[:, first : first + count], result[:], zero_s[:])
+                nc.vector.tensor_scalar_max(h[:, first : first + count], result[:], zero_block_0[:])
             else:
-                nc.scalar.activation(out=h[:, first : first + count], in_=result[:], func=RELU, bias=zero_s[:])
+                nc.scalar.activation(out=h[:, first : first + count], in_=result[:], func=RELU, bias=zero_block_0[:])
 
         def first_product(block):
             h = h_pool.tile([P, T], F32, name="h")
@@ -249,8 +251,8 @@ def tile_picked_gcn_mlp_relu_sub_l_kernel(
 
         def weave(turned, half, side):
             nc.scalar.copy(
-                out=z_grouped[half][side].bitcast(F32).rearrange("p (v u) -> p v u", u=2),
-                in_=turned[:].rearrange("p u v -> p v u"),
+                out=z_grouped[half][side].bitcast(F32).rearrange("p (c i u) -> p c u i", i=2, u=2),
+                in_=turned[:].rearrange("p u (c i) -> p c u i", i=2),
             )
 
 
@@ -269,8 +271,8 @@ def tile_picked_gcn_mlp_relu_sub_l_kernel(
         quantise_x(0)
         quantise_w1(0)
         copy_x(1, nc.vector.tensor_copy)
-        interleave(nc.vector.tensor_copy, x_grouped[2][:, 0:64, :], x_raw[2][:, :, 0:64])
-        interleave(nc.scalar.copy, x_grouped[2][:, 64:P, :], x_raw[2][:, :, 64:P])
+        interleave(nc.vector.tensor_copy, x_grouped[2][:, 0:X_VECTOR_SHARE, :], x_raw[2][:, :, 0:X_VECTOR_SHARE])
+        interleave(nc.scalar.copy, x_grouped[2][:, X_VECTOR_SHARE:P, :], x_raw[2][:, :, X_VECTOR_SHARE:P])
         quantise_x(1)
         quantise_x(2)
         first_product_of_block_0(0)
@@ -295,18 +297,18 @@ def tile_picked_gcn_mlp_relu_sub_l_kernel(
         for side in range(SIDES):
             turn(turned1[side], 1, side, 0)
         last = BLOCKS - 1
-        gs = [keep.tile([P, V], F32, align_bytes=64, name="last_g%d" % d) for d in range(1)]
-        for d in range(1):
+        gs = [keep.tile([P, V], F32, align_bytes=64, name="last_g%d" % d) for d in range(WHOLE_NEIGHBOURS)]
+        for d in range(WHOLE_NEIGHBOURS):
             gather(gs[d][:], last, d)
         totals = []
         for side in range(SIDES):
             total = psum_one.tile([P, P], F32, name="bank%d" % (6 + side))
             totals.append(total)
-        for d in range(1):
+        for d in range(WHOLE_NEIGHBOURS):
             for side in range(SIDES):
                 add_turned(totals[side][:], gs[d][:, P * side : P * (side + 1)], d)
         for side in range(SIDES):
-            for d in range(1, D):
+            for d in range(WHOLE_NEIGHBOURS, D):
                 g = keep.tile([P, P], F32, align_bytes=64, name="last_g%d_%d" % (d, side))
                 gather(g[:], last, d, P * side, P * (side + 1))
                 add_turned(totals[side][:], g[:], d)

@@ -19,6 +19,7 @@ U8 = mybir.dt.uint8
 FP8X4 = mybir.dt.float8_e4m3fn_x4
 MULT = mybir.AluOpType.mult
 RELU = mybir.ActivationFunctionType.Relu
+COPY = mybir.ActivationFunctionType.Copy
 
 X_PIECES = ((0, 256), (256, 128), (384, 128))
 
@@ -50,8 +51,8 @@ def tile_picked_gcn_mlp_relu_sub_l_kernel(
 
         lists = [keep.tile([P, V // 16], U16, name="list%d" % d) for d in range(D)]
         gate01 = keep.tile([P, 2, V], F32, align_bytes=64, name="gate01")
-        gate23 = keep.tile([P, 2, V], F32, name="gate23")
-        gates = [gate01[:, 0, :], gate01[:, 1, :], gate23[:, 0, :], gate23[:, 1, :]]
+        gate23 = keep.tile([P, 2, V], F32, align_bytes=64, name="gate23")
+        gates = [gate01[:, 0, :], gate01[:, 1, :]]
 
         x_raw = [load("x_raw0", xT[:, 0 : T // 2])[:]]
         w1_raw = [load_w1(0)]
@@ -60,14 +61,13 @@ def tile_picked_gcn_mlp_relu_sub_l_kernel(
         x_raw.append(x_rest[:, :, P : 2 * P])
         w1_raw.append(load_w1(1))
         nc.sync.dma_start(lists[0][:], pos1)
+        nc.sync.dma_start(lists[2][:], pos3)
         nc.sync.dma_start(out=gate01[:, 0, :], in_=gate[0])
+        nc.sync.dma_start(lists[3][:], pos4)
         w1_raw.append(load_w1(2))
         nc.sync.dma_start(lists[1][:], pos2)
         nc.sync.dma_start(out=gate01[:, 1, :], in_=gate[1])
-        nc.sync.dma_start(out=gate23[:, 0, :], in_=gate[2])
-        nc.sync.dma_start(lists[2][:], pos3)
-        nc.sync.dma_start(out=gate23[:, 1, :], in_=gate[3])
-        nc.sync.dma_start(lists[3][:], pos4)
+        nc.sync.dma_start(out=gate23[:], in_=gate[2:4].rearrange("d p v -> p d v"))
         for piece in range(3, len(W1_PIECES)):
             w1_raw.append(load_w1(piece))
         w2_raw = [load("w2_raw%d" % half, w2[P * PACK * half : P * PACK * (half + 1), :]) for half in range(HALVES)]
@@ -110,7 +110,7 @@ def tile_picked_gcn_mlp_relu_sub_l_kernel(
         w1_grouped = []
         w1_quantised = []
 
-        def copy_w1(piece, copy=nc.scalar.copy):
+        def copy_w1(piece, copy=nc.vector.tensor_copy):
             count = W1_PIECES[piece][1]
             grouped = keep.tile([P, count, PACK], BF16, align_bytes=64, name="w1_grouped%d" % piece)
             if count == P:
@@ -131,19 +131,13 @@ def tile_picked_gcn_mlp_relu_sub_l_kernel(
 
         w2_tiles = []
 
-        def copy_w2(half):
-            if half == 0:
-                w2_tiles.append(keep.tile([P, HALVES * N, PACK], BF16, align_bytes=64, name="w2_grouped"))
-            w2_grouped = w2_tiles[0]
-            interleave(nc.scalar.copy, w2_grouped[:, N * half : N * (half + 1), :], w2_raw[half][:])
+        def copy_w2(half, name):
+            grouped = keep.tile([P, N, PACK], BF16, align_bytes=64, name=name)
+            interleave(nc.vector.tensor_copy, grouped[:], w2_raw[half][:])
+            w2_tiles.append(grouped)
 
 
         h_tiles = []
-        zeros = {}
-        for block, name in ((1, "w1_grouped3"), (2, "w1_grouped4"), (3, "w1_grouped5"), (5, "w2_grouped")):
-            zeros[block] = keep.tile([P, 1], F32, align_bytes=64, name=name)
-            nc.gpsimd.memset(zeros[block][:], 0.0)
-
         zero_first = keep.tile([P, 1], F32, align_bytes=64, name="w1_grouped1")
         nc.gpsimd.memset(zero_first[:], 0.0)
         zero_block_0 = keep.tile([P, 1], F32, align_bytes=64, name="w1_grouped2")
@@ -173,23 +167,23 @@ def tile_picked_gcn_mlp_relu_sub_l_kernel(
             else:
                 nc.scalar.activation(out=h[:, first : first + count], in_=result[:], func=RELU, bias=zero_block_0[:])
 
+        products = [[] for block in range(BLOCKS)]
+
         def first_product(block):
-            h = h_pool.tile([P, T], F32, name="h")
             if block == 1:
                 for first, bank in ((0, "bank3"), (T // 2, "bank0")):
                     result = psum_one.tile([P, T // 2], F32, name=bank)
                     project(block, first, T // 2, result[:])
-                    if first == 0:
-                        nc.scalar.activation(out=h[:, 0 : T // 2], in_=result[:], func=RELU, bias=zeros[block][:])
-                    else:
-                        nc.scalar.activation(out=h[:, T // 2 : T], in_=result[:], func=RELU)
+                    products[block].append((first, T // 2, result))
             else:
                 result = psum_one.tile([P, T], F32, name="bank%d" % ((block - 1) % 4))
                 project(block, 0, T, result[:])
-                if block in zeros:
-                    nc.scalar.activation(out=h[:], in_=result[:], func=RELU, bias=zeros[block][:])
-                else:
-                    nc.scalar.activation(out=h[:], in_=result[:], func=RELU)
+                products[block].append((0, T, result))
+
+        def relu(block):
+            h = h_pool.tile([P, T], F32, name="h")
+            for first, count, result in products[block]:
+                nc.scalar.activation(out=h[:, first : first + count], in_=result[:], func=RELU)
             h_tiles.append(h)
 
 
@@ -222,15 +216,13 @@ def tile_picked_gcn_mlp_relu_sub_l_kernel(
                     in_=total.rearrange("v (p e) -> v p e", e=2),
                 )
 
-        def sum_block(block, gs):
-            sums = [
+        def fetch(g, block, d):
+            nc.scalar.activation(g, h_tiles[block][:].indirect(lists[d][:]), COPY)
+
+        def sum_banks(block):
+            return [
                 psum_one.tile([P, P], F32, name="bank%d" % (4 + 2 * (block % 2) + side)) for side in range(SIDES)
             ]
-            for d in range(D):
-                for side in range(SIDES):
-                    add_turned(sums[side][:], gs[d][:, P * side : P * (side + 1)], d)
-            for side in range(SIDES):
-                leave(block, side, sums[side][:])
 
 
         z0_grouped = keep.tile([P, SIDES, P * PACK], BF16, align_bytes=64, name="z0_grouped")
@@ -257,13 +249,15 @@ def tile_picked_gcn_mlp_relu_sub_l_kernel(
 
 
         steps = {
-            (0, 0): [(copy_w1, 3)],
-            (0, 1): [(quantise_w1, 2), (first_product, 2), (copy_w1, 4)],
-            (1, 1): [(quantise_w1, 3), (first_product, 3), (copy_w1, 5)],
+            (0, 0): [(copy_w1, 2)],
+            (0, 1): [(quantise_w1, 2), (first_product, 2)],
+            (1, 0): [(copy_w1, 3)],
+            (1, 1): [(quantise_w1, 3), (first_product, 3)],
+            (2, 0): [(copy_w1, 4)],
             (2, 1): [(quantise_w1, 4), (first_product, 4), (first_product, 5)],
-            (3, 1): [(quantise_w1, 5), (first_product, 6), (first_product, 7)],
-            (4, 2): [(turn_back, 0, 0, "bank3"), (turn_back, 0, 1, "bank0"), (copy_w2, 0)],
-            (5, 1): [(copy_w2, 1)],
+            (3, 0): [(copy_w2, 0, "w2_grouped0")],
+            (4, 0): [(copy_w1, 5)],
+            (4, 1): [(quantise_w1, 5), (first_product, 6), (first_product, 7)],
         }
 
         copy_x(0, nc.vector.tensor_copy)
@@ -280,52 +274,62 @@ def tile_picked_gcn_mlp_relu_sub_l_kernel(
         first_product_of_block_0(1)
         first_product_of_block_0(2)
         quantise_w1(1)
-        copy_w1(2)
         first_product(1)
 
-        for block in range(BLOCKS - 1):
-            gs = []
-            for d in range(D):
-                g = keep.tile([P, V], F32, name="g%d_%d" % (block, d))
+        last = BLOCKS - 1
+        sums = []
+        turned1 = []
+        for block in range(BLOCKS):
+            sums.append(sum_banks(block))
+            fetched = keep.tile([P, 2, V], F32, align_bytes=64, name="fetched%d" % block)
+            for d in range(2):
+                fetch(fetched[:, d, :], block, 2 + d)
+            if block < last:
+                relu(block + 1)
+            if block > 0:
+                for side in range(SIDES):
+                    leave(block - 1, side, sums[block - 1][side][:])
+            if block == 5:
+                turn_back(0, 0, "bank3")
+                turn_back(0, 1, "bank0")
+            for d in range(2):
+                g = keep.tile([P, V], F32, align_bytes=64, name="g%d_%d" % (block, d))
                 gather(g[:], block, d)
-                gs.append(g)
+                for side in range(SIDES):
+                    add_turned(sums[block][side][:], g[:, P * side : P * (side + 1)], d)
                 for step in steps.get((block, d), []):
                     step[0](*step[1:])
-            sum_block(block, gs)
-
-        turned1 = [psum_one.tile([P, 2, P], F32, name=bank) for bank in ("bank0", "bank4")]
-        for side in range(SIDES):
-            turn(turned1[side], 1, side, 0)
-        last = BLOCKS - 1
-        gs = [keep.tile([P, V], F32, align_bytes=64, name="last_g%d" % d) for d in range(WHOLE_NEIGHBOURS)]
-        for d in range(WHOLE_NEIGHBOURS):
-            gather(gs[d][:], last, d)
-        totals = []
-        for side in range(SIDES):
-            total = psum_one.tile([P, P], F32, name="bank%d" % (6 + side))
-            totals.append(total)
-        for d in range(WHOLE_NEIGHBOURS):
-            for side in range(SIDES):
-                add_turned(totals[side][:], gs[d][:, P * side : P * (side + 1)], d)
-        for side in range(SIDES):
-            for d in range(WHOLE_NEIGHBOURS, D):
-                g = keep.tile([P, P], F32, align_bytes=64, name="last_g%d_%d" % (d, side))
-                gather(g[:], last, d, P * side, P * (side + 1))
-                add_turned(totals[side][:], g[:], d)
-            leave(last, side, totals[side][:])
+            if block < last:
+                gated = keep.tile([P, 2, V], F32, name="gated%d" % block)
+                nc.vector.tensor_tensor(gated[:], fetched[:], gate23[:], MULT)
+                for d in range(2):
+                    for side in range(SIDES):
+                        add_turned(sums[block][side][:], gated[:, d, P * side : P * (side + 1)], 2 + d)
+            else:
+                for side, bank in enumerate(("bank0", "bank4")):
+                    turned1.append(psum_one.tile([P, 2, P], F32, name=bank))
+                    turn(turned1[side], 1, side, 0)
+                for side in range(SIDES):
+                    targets = slice(P * side, P * (side + 1))
+                    gated = keep.tile([P, 2, P], F32, align_bytes=64, name="last_gated%d" % side)
+                    nc.vector.tensor_tensor(gated[:], fetched[:, :, targets], gate23[:, :, targets], MULT)
+                    for d in range(2):
+                        add_turned(sums[block][side][:], gated[:, d, :], 2 + d)
+                    leave(block, side, sums[block][side][:])
         for side in range(SIDES):
             turn(turned1[side], 1, side, 1)
             weave(turned1[side], 1, side)
 
-        w2_quantised = [operand("w2_0", N, "last_g3_1"), operand("w2_1", N, "gate01")]
+        w2_quantised = [operand("w2_0", N, "last_gated1"), operand("w2_1", N)]
 
         def quantise_w2(half):
-            grouped = w2_tiles[0][:, N * half : N * (half + 1), :].rearrange("p w j -> p (w j)")
+            grouped = w2_tiles[half][:].rearrange("p w j -> p (w j)")
             quantise(w2_quantised[half][0][:], w2_quantised[half][1][:], grouped)
 
-        quantise_w2(1)
-        z0_codes, z0_scales = operand("z0", V, "last_g0")
+        copy_w2(1, "gate23")
+        z0_codes, z0_scales = operand("z0", V, "fetched%d" % last)
         quantise(z0_codes[:], z0_scales[:], z0_grouped[:].rearrange("p s w -> p (s w)"))
+        quantise_w2(1)
         quantise_w2(0)
         z1 = [operand("z1_%d" % side, P) for side in range(SIDES)]
         for side in range(SIDES):

@@ -25,7 +25,7 @@ X_PIECES = ((0, 256), (256, 128), (384, 128))
 
 X_VECTOR_SHARE = 64
 
-W1_PIECES = ((0, 128), (128, 128), (256, 128), (384, 128), (512, 256), (768, 256))
+W1_PIECES = ((0, 128), (128, 128), (256, 256), (512, 256), (768, 256))
 
 WHOLE_NEIGHBOURS = 2
 
@@ -111,9 +111,9 @@ def tile_picked_gcn_mlp_relu_sub_l_kernel(
         w1_quantised = []
 
         def copy_w1(piece, copy=nc.vector.tensor_copy):
-            count = W1_PIECES[piece][1]
+            first, count = W1_PIECES[piece]
             grouped = keep.tile([P, count, PACK], BF16, align_bytes=64, name="w1_grouped%d" % piece)
-            if count == P:
+            if first < P * PACK:
                 interleave(copy, grouped[:], w1_raw[piece][:])
             else:
                 copy(
@@ -250,14 +250,12 @@ def tile_picked_gcn_mlp_relu_sub_l_kernel(
 
         steps = {
             (0, 0): [(copy_w1, 2)],
-            (0, 1): [(quantise_w1, 2), (first_product, 2)],
+            (0, 1): [(quantise_w1, 2), (first_product, 2), (first_product, 3)],
             (1, 0): [(copy_w1, 3)],
-            (1, 1): [(quantise_w1, 3), (first_product, 3)],
+            (1, 1): [(quantise_w1, 3), (first_product, 4), (first_product, 5)],
             (2, 0): [(copy_w1, 4)],
-            (2, 1): [(quantise_w1, 4), (first_product, 4), (first_product, 5)],
+            (2, 1): [(quantise_w1, 4), (first_product, 6), (first_product, 7)],
             (3, 0): [(copy_w2, 0, "w2_grouped0")],
-            (4, 0): [(copy_w1, 5)],
-            (4, 1): [(quantise_w1, 5), (first_product, 6), (first_product, 7)],
         }
 
         copy_x(0, nc.vector.tensor_copy)
@@ -284,12 +282,16 @@ def tile_picked_gcn_mlp_relu_sub_l_kernel(
             fetched = keep.tile([P, 2, V], F32, align_bytes=64, name="fetched%d" % block)
             for d in range(2):
                 fetch(fetched[:, d, :], block, 2 + d)
-            if block < last:
-                relu(block + 1)
+            if block == 0:
+                relu(1)
+            elif 2 * block < BLOCKS:
+                relu(2 * block)
             if block > 0:
                 for side in range(SIDES):
                     leave(block - 1, side, sums[block - 1][side][:])
-            if block == 5:
+            if 0 < 2 * block < BLOCKS:
+                relu(2 * block + 1)
+            if block == 4:
                 turn_back(0, 0, "bank3")
                 turn_back(0, 1, "bank0")
             for d in range(2):

@@ -131,9 +131,9 @@ def tile_picked_gcn_mlp_relu_sub_l_kernel(
 
         w2_tiles = []
 
-        def copy_w2(half, name):
+        def copy_w2(half, name, copy):
             grouped = keep.tile([P, N, PACK], BF16, align_bytes=64, name=name)
-            interleave(nc.vector.tensor_copy, grouped[:], w2_raw[half][:])
+            interleave(copy, grouped[:], w2_raw[half][:])
             w2_tiles.append(grouped)
 
 
@@ -199,8 +199,15 @@ def tile_picked_gcn_mlp_relu_sub_l_kernel(
                 MULT,
             )
 
-        def add_turned(total, g, d):
-            nc.tensor.matmul(total, lhsT=g, rhs=identity[:], start=(d == 0), stop=(d == D - 1), is_transpose=True)
+        def add_turned(total, g, turn_number):
+            nc.tensor.matmul(
+                total,
+                lhsT=g,
+                rhs=identity[:],
+                start=(turn_number == 0),
+                stop=(turn_number == D - 1),
+                is_transpose=True,
+            )
 
         def leave(block, side, total):
             half, quarter = divmod(block, PACK)
@@ -220,9 +227,13 @@ def tile_picked_gcn_mlp_relu_sub_l_kernel(
             nc.scalar.activation(g, h_tiles[block][:].indirect(lists[d][:]), COPY)
 
         def sum_banks(block):
-            return [
-                psum_one.tile([P, P], F32, name="bank%d" % (4 + 2 * (block % 2) + side)) for side in range(SIDES)
-            ]
+            if block == BLOCKS - 2:
+                names = ("bank0", "bank3")
+            elif block == BLOCKS - 1:
+                names = ("bank4", "bank5")
+            else:
+                names = ("bank%d" % (4 + 2 * (block % 2)), "bank%d" % (5 + 2 * (block % 2)))
+            return [psum_one.tile([P, P], F32, name=name) for name in names]
 
 
         z0_grouped = keep.tile([P, SIDES, P * PACK], BF16, align_bytes=64, name="z0_grouped")
@@ -255,7 +266,6 @@ def tile_picked_gcn_mlp_relu_sub_l_kernel(
             (1, 1): [(quantise_w1, 3), (first_product, 4), (first_product, 5)],
             (2, 0): [(copy_w1, 4)],
             (2, 1): [(quantise_w1, 4), (first_product, 6), (first_product, 7)],
-            (3, 0): [(copy_w2, 0, "w2_grouped0")],
         }
 
         copy_x(0, nc.vector.tensor_copy)
@@ -291,45 +301,44 @@ def tile_picked_gcn_mlp_relu_sub_l_kernel(
                     leave(block - 1, side, sums[block - 1][side][:])
             if 0 < 2 * block < BLOCKS:
                 relu(2 * block + 1)
-            if block == 4:
-                turn_back(0, 0, "bank3")
-                turn_back(0, 1, "bank0")
-            for d in range(2):
+            if block == last:
+                turn_back(0, 0, "bank1")
+                turn_back(0, 1, "bank2")
+                copy_w2(0, "w2_grouped0", nc.scalar.copy)
+            whole = 2 if block < last else 1
+            for d in range(whole):
                 g = keep.tile([P, V], F32, align_bytes=64, name="g%d_%d" % (block, d))
                 gather(g[:], block, d)
                 for side in range(SIDES):
                     add_turned(sums[block][side][:], g[:, P * side : P * (side + 1)], d)
                 for step in steps.get((block, d), []):
                     step[0](*step[1:])
-            if block < last:
-                gated = keep.tile([P, 2, V], F32, name="gated%d" % block)
-                nc.vector.tensor_tensor(gated[:], fetched[:], gate23[:], MULT)
-                for d in range(2):
-                    for side in range(SIDES):
-                        add_turned(sums[block][side][:], gated[:, d, P * side : P * (side + 1)], 2 + d)
-            else:
-                for side, bank in enumerate(("bank0", "bank4")):
+            if block == last:
+                for side, bank in enumerate(("bank6", "bank7")):
                     turned1.append(psum_one.tile([P, 2, P], F32, name=bank))
                     turn(turned1[side], 1, side, 0)
+            gated = keep.tile([P, 2, V], F32, name="gated%d" % block)
+            nc.vector.tensor_tensor(gated[:], fetched[:], gate23[:], MULT)
+            for d in range(2):
                 for side in range(SIDES):
-                    targets = slice(P * side, P * (side + 1))
-                    gated = keep.tile([P, 2, P], F32, align_bytes=64, name="last_gated%d" % side)
-                    nc.vector.tensor_tensor(gated[:], fetched[:, :, targets], gate23[:, :, targets], MULT)
-                    for d in range(2):
-                        add_turned(sums[block][side][:], gated[:, d, :], 2 + d)
-                    leave(block, side, sums[block][side][:])
+                    add_turned(sums[block][side][:], gated[:, d, P * side : P * (side + 1)], whole + d)
+        for side in range(SIDES):
+            g = keep.tile([P, P], F32, align_bytes=64, name="last_g%d" % side)
+            gather(g[:], last, 1, P * side, P * (side + 1))
+            add_turned(sums[last][side][:], g[:], D - 1)
+            leave(last, side, sums[last][side][:])
         for side in range(SIDES):
             turn(turned1[side], 1, side, 1)
             weave(turned1[side], 1, side)
 
-        w2_quantised = [operand("w2_0", N, "last_gated1"), operand("w2_1", N)]
+        w2_quantised = [operand("w2_0", N, "last_g1"), operand("w2_1", N)]
 
         def quantise_w2(half):
             grouped = w2_tiles[half][:].rearrange("p w j -> p (w j)")
             quantise(w2_quantised[half][0][:], w2_quantised[half][1][:], grouped)
 
-        copy_w2(1, "gate23")
-        z0_codes, z0_scales = operand("z0", V, "fetched%d" % last)
+        copy_w2(1, "gate01", nc.vector.tensor_copy)
+        z0_codes, z0_scales = operand("z0", V, "last_g0")
         quantise(z0_codes[:], z0_scales[:], z0_grouped[:].rearrange("p s w -> p (s w)"))
         quantise_w2(1)
         quantise_w2(0)
@@ -352,7 +361,7 @@ def tile_picked_gcn_mlp_relu_sub_l_kernel(
 
         banks = [
             [psum_one.tile([P, P], F32, name="bank%d" % (1 + rows)) for rows in range(N // P)],
-            [psum_one.tile([P, P], F32, name="bank%d" % (3 + 2 * rows)) for rows in range(N // P)],
+            [psum_one.tile([P, P], F32, name="bank%d" % (3 * rows)) for rows in range(N // P)],
         ]
         for side in range(SIDES):
             targets = slice(P * side, P * (side + 1))

@@ -338,10 +338,10 @@ def tile_picked_gcn_mlp_relu_sub_l_kernel(
             quantise(w2_quantised[half][0][:], w2_quantised[half][1][:], grouped)
 
         copy_w2(1, "gate01", nc.vector.tensor_copy)
+        quantise_w2(0)
         z0_codes, z0_scales = operand("z0", V, "last_g0")
         quantise(z0_codes[:], z0_scales[:], z0_grouped[:].rearrange("p s w -> p (s w)"))
         quantise_w2(1)
-        quantise_w2(0)
         z1 = [operand("z1_%d" % side, P) for side in range(SIDES)]
         for side in range(SIDES):
             quantise(z1[side][0][:], z1[side][1][:], z1_grouped[side][:])

@@ -27,7 +27,9 @@ X_VECTOR_SHARE = 64
 
 W1_PIECES = ((0, 128), (128, 128), (256, 256), (512, 256), (768, 256))
 
-WHOLE_NEIGHBOURS = 2
+FUSED = 2
+
+LAST = BLOCKS - 1
 
 
 def tile_picked_gcn_mlp_relu_sub_l_kernel(
@@ -96,8 +98,8 @@ def tile_picked_gcn_mlp_relu_sub_l_kernel(
         ]
         x_codes, x_scales = operand("x", T)
 
-        def copy_x(piece, copy):
-            interleave(copy, x_grouped[piece][:], x_raw[piece])
+        def copy_x(piece):
+            interleave(nc.vector.tensor_copy, x_grouped[piece][:], x_raw[piece])
 
         def quantise_x(piece):
             first, count = X_PIECES[piece]
@@ -110,13 +112,13 @@ def tile_picked_gcn_mlp_relu_sub_l_kernel(
         w1_grouped = []
         w1_quantised = []
 
-        def copy_w1(piece, copy=nc.vector.tensor_copy):
+        def copy_w1(piece):
             first, count = W1_PIECES[piece]
             grouped = keep.tile([P, count, PACK], BF16, align_bytes=64, name="w1_grouped%d" % piece)
             if first < P * PACK:
-                interleave(copy, grouped[:], w1_raw[piece][:])
+                interleave(nc.vector.tensor_copy, grouped[:], w1_raw[piece][:])
             else:
-                copy(
+                nc.vector.tensor_copy(
                     out=grouped[:].rearrange("p (u c e) j -> p c j u e", u=2, e=2),
                     in_=w1_raw[piece][:].rearrange("p j (c u e) -> p c j u e", u=2, e=2),
                 )
@@ -129,12 +131,12 @@ def tile_picked_gcn_mlp_relu_sub_l_kernel(
             for column in range(0, count, P):
                 w1_quantised.append((codes, scales, column))
 
-        w2_tiles = []
+        w2_grouped = []
 
         def copy_w2(half, name, copy):
             grouped = keep.tile([P, N, PACK], BF16, align_bytes=64, name=name)
             interleave(copy, grouped[:], w2_raw[half][:])
-            w2_tiles.append(grouped)
+            w2_grouped.append(grouped)
 
 
         h_tiles = []
@@ -191,11 +193,11 @@ def tile_picked_gcn_mlp_relu_sub_l_kernel(
         summed1 = [keep.tile([P, 2, P, 2], BF16, align_bytes=64, name="summed1_%d" % side) for side in range(SIDES)]
         summed = [[summed0[:, side] for side in range(SIDES)], [summed1[side][:] for side in range(SIDES)]]
 
-        def gather(g, block, d, first=0, last=V):
+        def gather(g, block, d, first=0, end=V):
             nc.vector.tensor_tensor(
                 g,
-                h_tiles[block][:].indirect(lists[d][:, first // 16 : last // 16]),
-                gates[d][:, first:last],
+                h_tiles[block][:].indirect(lists[d][:, first // 16 : end // 16]),
+                gates[d][:, first:end],
                 MULT,
             )
 
@@ -217,9 +219,9 @@ def tile_picked_gcn_mlp_relu_sub_l_kernel(
                     in_=total.rearrange("v (p u e) -> v u p e", u=2, e=2),
                 )
             else:
-                piece, u = divmod(quarter, 2)
+                pair, u = divmod(quarter, 2)
                 nc.scalar.copy(
-                    out=summed[half][side][:, u, 64 * piece : 64 * (piece + 1), :],
+                    out=summed[half][side][:, u, 64 * pair : 64 * (pair + 1), :],
                     in_=total.rearrange("v (p e) -> v p e", e=2),
                 )
 
@@ -227,9 +229,9 @@ def tile_picked_gcn_mlp_relu_sub_l_kernel(
             nc.scalar.activation(g, h_tiles[block][:].indirect(lists[d][:]), COPY)
 
         def sum_banks(block):
-            if block == BLOCKS - 2:
+            if block == LAST - 1:
                 names = ("bank0", "bank3")
-            elif block == BLOCKS - 1:
+            elif block == LAST:
                 names = ("bank4", "bank5")
             else:
                 names = ("bank%d" % (4 + 2 * (block % 2)), "bank%d" % (5 + 2 * (block % 2)))
@@ -259,74 +261,76 @@ def tile_picked_gcn_mlp_relu_sub_l_kernel(
             )
 
 
-        steps = {
-            (0, 0): [(copy_w1, 2)],
-            (0, 1): [(quantise_w1, 2), (first_product, 2), (first_product, 3)],
-            (1, 0): [(copy_w1, 3)],
-            (1, 1): [(quantise_w1, 3), (first_product, 4), (first_product, 5)],
-            (2, 0): [(copy_w1, 4)],
-            (2, 1): [(quantise_w1, 4), (first_product, 6), (first_product, 7)],
-        }
-
-        copy_x(0, nc.vector.tensor_copy)
-        copy_w1(0, nc.vector.tensor_copy)
+        copy_x(0)
+        copy_w1(0)
         quantise_x(0)
         quantise_w1(0)
-        copy_x(1, nc.vector.tensor_copy)
+        copy_x(1)
         interleave(nc.vector.tensor_copy, x_grouped[2][:, 0:X_VECTOR_SHARE, :], x_raw[2][:, :, 0:X_VECTOR_SHARE])
         interleave(nc.scalar.copy, x_grouped[2][:, X_VECTOR_SHARE:P, :], x_raw[2][:, :, X_VECTOR_SHARE:P])
         quantise_x(1)
         quantise_x(2)
         first_product_of_block_0(0)
-        copy_w1(1, nc.vector.tensor_copy)
+        copy_w1(1)
         first_product_of_block_0(1)
         first_product_of_block_0(2)
         quantise_w1(1)
         first_product(1)
 
-        last = BLOCKS - 1
         sums = []
         turned1 = []
         for block in range(BLOCKS):
+            piece = block + 2
+            makes_pair = piece < len(W1_PIECES)
+            empties_pair = 0 < 2 * block < BLOCKS
+
+            fetched = keep.tile([P, D - FUSED, V], F32, align_bytes=64, name="fetched%d" % block)
+            for d in range(FUSED, D):
+                fetch(fetched[:, d - FUSED, :], block, d)
+            if block > 1:
+                for side in range(SIDES):
+                    leave(block - 2, side, sums[block - 2][side][:])
             sums.append(sum_banks(block))
-            fetched = keep.tile([P, 2, V], F32, align_bytes=64, name="fetched%d" % block)
-            for d in range(2):
-                fetch(fetched[:, d, :], block, 2 + d)
             if block == 0:
                 relu(1)
-            elif 2 * block < BLOCKS:
+            if empties_pair:
                 relu(2 * block)
-            if block > 0:
+            if empties_pair:
+                relu(2 * block + 1)
+            if block == LAST:
                 for side in range(SIDES):
                     leave(block - 1, side, sums[block - 1][side][:])
-            if 0 < 2 * block < BLOCKS:
-                relu(2 * block + 1)
-            if block == last:
                 turn_back(0, 0, "bank1")
                 turn_back(0, 1, "bank2")
                 copy_w2(0, "w2_grouped0", nc.scalar.copy)
-            whole = 2 if block < last else 1
+
+            whole = FUSED if block < LAST else FUSED - 1
             for d in range(whole):
                 g = keep.tile([P, V], F32, align_bytes=64, name="g%d_%d" % (block, d))
                 gather(g[:], block, d)
                 for side in range(SIDES):
                     add_turned(sums[block][side][:], g[:, P * side : P * (side + 1)], d)
-                for step in steps.get((block, d), []):
-                    step[0](*step[1:])
-            if block == last:
+                if makes_pair and d == 0:
+                    copy_w1(piece)
+                if makes_pair and d == 1:
+                    quantise_w1(piece)
+                    first_product(2 * block + 2)
+                    first_product(2 * block + 3)
+            if block == LAST:
                 for side, bank in enumerate(("bank6", "bank7")):
                     turned1.append(psum_one.tile([P, 2, P], F32, name=bank))
                     turn(turned1[side], 1, side, 0)
-            gated = keep.tile([P, 2, V], F32, name="gated%d" % block)
+            gated = keep.tile([P, D - FUSED, V], F32, name="gated%d" % block)
             nc.vector.tensor_tensor(gated[:], fetched[:], gate23[:], MULT)
-            for d in range(2):
+            for j in range(D - FUSED):
                 for side in range(SIDES):
-                    add_turned(sums[block][side][:], gated[:, d, P * side : P * (side + 1)], whole + d)
+                    add_turned(sums[block][side][:], gated[:, j, P * side : P * (side + 1)], whole + j)
+
         for side in range(SIDES):
             g = keep.tile([P, P], F32, align_bytes=64, name="last_g%d" % side)
-            gather(g[:], last, 1, P * side, P * (side + 1))
-            add_turned(sums[last][side][:], g[:], D - 1)
-            leave(last, side, sums[last][side][:])
+            gather(g[:], LAST, 1, P * side, P * (side + 1))
+            add_turned(sums[LAST][side][:], g[:], D - 1)
+            leave(LAST, side, sums[LAST][side][:])
         for side in range(SIDES):
             turn(turned1[side], 1, side, 1)
             weave(turned1[side], 1, side)
@@ -334,7 +338,7 @@ def tile_picked_gcn_mlp_relu_sub_l_kernel(
         w2_quantised = [operand("w2_0", N, "last_g1"), operand("w2_1", N)]
 
         def quantise_w2(half):
-            grouped = w2_tiles[half][:].rearrange("p w j -> p (w j)")
+            grouped = w2_grouped[half][:].rearrange("p w j -> p (w j)")
             quantise(w2_quantised[half][0][:], w2_quantised[half][1][:], grouped)
 
         copy_w2(1, "gate01", nc.vector.tensor_copy)
@@ -360,8 +364,8 @@ def tile_picked_gcn_mlp_relu_sub_l_kernel(
             )
 
         banks = [
-            [psum_one.tile([P, P], F32, name="bank%d" % (1 + rows)) for rows in range(N // P)],
-            [psum_one.tile([P, P], F32, name="bank%d" % (3 * rows)) for rows in range(N // P)],
+            [psum_one.tile([P, P], F32, name=name) for name in names]
+            for names in (("bank1", "bank2"), ("bank0", "bank3"))
         ]
         for side in range(SIDES):
             targets = slice(P * side, P * (side + 1))
@@ -377,6 +381,6 @@ def tile_picked_gcn_mlp_relu_sub_l_kernel(
             copies[rows](out=stored0[:, rows, :], in_=banks[0][rows][:])
         nc.sync.dma_start(out=out[:, 0:P].rearrange("(r p) v -> p r v", p=P), in_=stored0[:])
         for rows, queue in enumerate((nc.sync, nc.scalar)):
-            result = keep.tile([P, P], F32, name="stored1_%d" % rows)
-            copies[rows](out=result[:], in_=banks[1][rows][:])
-            queue.dma_start(out=out[P * rows : P * (rows + 1), P:V], in_=result[:])
+            stored1 = keep.tile([P, P], F32, name="stored1_%d" % rows)
+            copies[rows](out=stored1[:], in_=banks[1][rows][:])
+            queue.dma_start(out=out[P * rows : P * (rows + 1), P:V], in_=stored1[:])

@@ -27,6 +27,8 @@ X_VECTOR_SHARE = 64
 
 W1_PIECES = ((0, 128), (128, 128), (256, 256), (512, 256), (768, 256))
 
+PIECE_BLOCKS = ((0,), (1,), (2, 3), (4, 6), (5, 7))
+
 FUSED = 2
 
 LAST = BLOCKS - 1
@@ -110,7 +112,7 @@ def tile_picked_gcn_mlp_relu_sub_l_kernel(
             )
 
         w1_grouped = []
-        w1_quantised = []
+        w1_quantised = {}
 
         def copy_w1(piece):
             first, count = W1_PIECES[piece]
@@ -128,8 +130,8 @@ def tile_picked_gcn_mlp_relu_sub_l_kernel(
             count = W1_PIECES[piece][1]
             codes, scales = operand("w1_%d" % piece, count)
             quantise(codes[:], scales[:], w1_grouped[piece][:].rearrange("p w j -> p (w j)"))
-            for column in range(0, count, P):
-                w1_quantised.append((codes, scales, column))
+            for i, block in enumerate(PIECE_BLOCKS[piece]):
+                w1_quantised[block] = (codes, scales, P * i)
 
         w2_grouped = []
 
@@ -139,7 +141,7 @@ def tile_picked_gcn_mlp_relu_sub_l_kernel(
             w2_grouped.append(grouped)
 
 
-        h_tiles = []
+        h_tiles = {}
         zero_first = keep.tile([P, 1], F32, align_bytes=64, name="w1_grouped1")
         nc.gpsimd.memset(zero_first[:], 0.0)
         zero_block_0 = keep.tile([P, 1], F32, align_bytes=64, name="w1_grouped2")
@@ -159,7 +161,7 @@ def tile_picked_gcn_mlp_relu_sub_l_kernel(
 
         def first_product_of_block_0(piece):
             if piece == 0:
-                h_tiles.append(h_pool.tile([P, T], F32, name="h"))
+                h_tiles[0] = h_pool.tile([P, T], F32, name="h")
             h = h_tiles[0]
             first, count = X_PIECES[piece]
             result = psum_one.tile([P, count], F32, name="bank%d" % piece)
@@ -178,7 +180,7 @@ def tile_picked_gcn_mlp_relu_sub_l_kernel(
                     project(block, first, T // 2, result[:])
                     products[block].append((first, T // 2, result))
             else:
-                result = psum_one.tile([P, T], F32, name="bank%d" % ((block - 1) % 4))
+                result = psum_one.tile([P, T], F32, name="bank%d" % {2: 1, 3: 2, 4: 3, 6: 0, 5: 1, 7: 2}[block])
                 project(block, 0, T, result[:])
                 products[block].append((0, T, result))
 
@@ -186,12 +188,14 @@ def tile_picked_gcn_mlp_relu_sub_l_kernel(
             h = h_pool.tile([P, T], F32, name="h")
             for first, count, result in products[block]:
                 nc.scalar.activation(out=h[:, first : first + count], in_=result[:], func=RELU)
-            h_tiles.append(h)
+            h_tiles[block] = h
 
 
         summed0 = keep.tile([P, SIDES, 2, P, 2], BF16, align_bytes=64, name="summed0")
-        summed1 = [keep.tile([P, 2, P, 2], BF16, align_bytes=64, name="summed1_%d" % side) for side in range(SIDES)]
-        summed = [[summed0[:, side] for side in range(SIDES)], [summed1[side][:] for side in range(SIDES)]]
+        summed1 = [
+            [keep.tile([P, P, 2], BF16, align_bytes=64, name="summed1_%d_%d" % (side, u)) for u in range(2)]
+            for side in range(SIDES)
+        ]
 
         def gather(g, block, d, first=0, end=V):
             nc.vector.tensor_tensor(
@@ -215,13 +219,13 @@ def tile_picked_gcn_mlp_relu_sub_l_kernel(
             half, quarter = divmod(block, PACK)
             if half == 0:
                 nc.scalar.copy(
-                    out=summed[half][side][:, :, 32 * quarter : 32 * (quarter + 1), :],
+                    out=summed0[:, side, :, 32 * quarter : 32 * (quarter + 1), :],
                     in_=total.rearrange("v (p u e) -> v u p e", u=2, e=2),
                 )
             else:
-                pair, u = divmod(quarter, 2)
+                u, pair = divmod(quarter, 2)
                 nc.scalar.copy(
-                    out=summed[half][side][:, u, 64 * pair : 64 * (pair + 1), :],
+                    out=summed1[side][u][:, 64 * pair : 64 * (pair + 1), :],
                     in_=total.rearrange("v (p e) -> v p e", e=2),
                 )
 
@@ -245,7 +249,8 @@ def tile_picked_gcn_mlp_relu_sub_l_kernel(
         z_grouped = [[z0_grouped[:, side, :] for side in range(SIDES)], [z1_grouped[side][:] for side in range(SIDES)]]
 
         def turn(turned, half, side, u):
-            words = summed[half][side][:, u].rearrange("v p e -> v (p e)").bitcast(F32)
+            pairs = summed0[:, side, u] if half == 0 else summed1[side][u][:]
+            words = pairs.rearrange("v p e -> v (p e)").bitcast(F32)
             nc.tensor.transpose(turned[:, u, :], words, identity[:])
 
         def turn_back(half, side, bank):
@@ -294,9 +299,8 @@ def tile_picked_gcn_mlp_relu_sub_l_kernel(
             if block == 0:
                 relu(1)
             if empties_pair:
-                relu(2 * block)
-            if empties_pair:
-                relu(2 * block + 1)
+                for other in PIECE_BLOCKS[block + 1]:
+                    relu(other)
             if block == LAST:
                 for side in range(SIDES):
                     leave(block - 1, side, sums[block - 1][side][:])
@@ -314,8 +318,8 @@ def tile_picked_gcn_mlp_relu_sub_l_kernel(
                     copy_w1(piece)
                 if makes_pair and d == 1:
                     quantise_w1(piece)
-                    first_product(2 * block + 2)
-                    first_product(2 * block + 3)
+                    for other in PIECE_BLOCKS[piece]:
+                        first_product(other)
             if block == LAST:
                 for side, bank in enumerate(("bank6", "bank7")):
                     turned1.append(psum_one.tile([P, 2, P], F32, name=bank))

@@ -307,6 +307,8 @@ def tile_picked_gcn_mlp_relu_sub_l_kernel(
                 turn_back(0, 0, "bank1")
                 turn_back(0, 1, "bank2")
                 copy_w2(0, "w2_grouped0", nc.scalar.copy)
+                w2_left = keep.tile([P, P, PACK], BF16, align_bytes=64, name="fetched5")
+                interleave(nc.scalar.copy, w2_left[:], w2_raw[1][:, :, 0:P])
 
             whole = FUSED if block < LAST else FUSED - 1
             for d in range(whole):
@@ -341,15 +343,17 @@ def tile_picked_gcn_mlp_relu_sub_l_kernel(
 
         w2_quantised = [operand("w2_0", N, "last_g1"), operand("w2_1", N)]
 
-        def quantise_w2(half):
-            grouped = w2_grouped[half][:].rearrange("p w j -> p (w j)")
-            quantise(w2_quantised[half][0][:], w2_quantised[half][1][:], grouped)
+        def quantise_w2(half, columns, grouped):
+            codes, scales = w2_quantised[half]
+            quantise(codes[:, columns], scales[:, columns], grouped[:].rearrange("p w j -> p (w j)"))
 
-        copy_w2(1, "gate01", nc.vector.tensor_copy)
-        quantise_w2(0)
+        w2_right = keep.tile([P, P, PACK], BF16, align_bytes=64, name="gate01")
+        interleave(nc.vector.tensor_copy, w2_right[:], w2_raw[1][:, :, P:N])
+        quantise_w2(0, slice(0, N), w2_grouped[0])
         z0_codes, z0_scales = operand("z0", V, "last_g0")
         quantise(z0_codes[:], z0_scales[:], z0_grouped[:].rearrange("p s w -> p (s w)"))
-        quantise_w2(1)
+        quantise_w2(1, slice(P, N), w2_right)
+        quantise_w2(1, slice(0, P), w2_left)
         z1 = [operand("z1_%d" % side, P) for side in range(SIDES)]
         for side in range(SIDES):
             quantise(z1[side][0][:], z1[side][1][:], z1_grouped[side][:])

@@ -32,6 +32,7 @@ PIECE_BLOCKS = ((0,), (1,), (2, 3), (4, 6), (5, 7))
 FUSED = 2
 
 LAST = BLOCKS - 1
+SUM_BANKS = ((4, 5), (6, 7), (4, 5), (6, 7), (3, 0), (4, 5), (1, 2), (3, 0))
 
 
 def tile_picked_gcn_mlp_relu_sub_l_kernel(
@@ -233,12 +234,7 @@ def tile_picked_gcn_mlp_relu_sub_l_kernel(
             nc.scalar.activation(g, h_tiles[block][:].indirect(lists[d][:]), COPY)
 
         def sum_banks(block):
-            if block == LAST - 1:
-                names = ("bank0", "bank3")
-            elif block == LAST:
-                names = ("bank4", "bank5")
-            else:
-                names = ("bank%d" % (4 + 2 * (block % 2)), "bank%d" % (5 + 2 * (block % 2)))
+            names = ["bank%d" % bank for bank in SUM_BANKS[block]]
             return [psum_one.tile([P, P], F32, name=name) for name in names]
 
 
@@ -304,8 +300,8 @@ def tile_picked_gcn_mlp_relu_sub_l_kernel(
             if block == LAST:
                 for side in range(SIDES):
                     leave(block - 1, side, sums[block - 1][side][:])
-                turn_back(0, 0, "bank1")
-                turn_back(0, 1, "bank2")
+                turn_back(0, 0, "bank6")
+                turn_back(0, 1, "bank7")
                 copy_w2(0, "w2_grouped0", nc.scalar.copy)
                 w2_left = keep.tile([P, P, PACK], BF16, align_bytes=64, name="fetched5")
                 interleave(nc.scalar.copy, w2_left[:], w2_raw[1][:, :, 0:P])
@@ -323,7 +319,7 @@ def tile_picked_gcn_mlp_relu_sub_l_kernel(
                     for other in PIECE_BLOCKS[piece]:
                         first_product(other)
             if block == LAST:
-                for side, bank in enumerate(("bank6", "bank7")):
+                for side, bank in enumerate(("bank4", "bank5")):
                     turned1.append(psum_one.tile([P, 2, P], F32, name=bank))
                     turn(turned1[side], 1, side, 0)
             gated = keep.tile([P, D - FUSED, V], F32, name="gated%d" % block)
@@ -373,7 +369,7 @@ def tile_picked_gcn_mlp_relu_sub_l_kernel(
 
         banks = [
             [psum_one.tile([P, P], F32, name=name) for name in names]
-            for names in (("bank1", "bank2"), ("bank0", "bank3"))
+            for names in (("bank6", "bank7"), ("bank1", "bank2"))
         ]
         for side in range(SIDES):
             targets = slice(P * side, P * (side + 1))

from contextlib import ExitStack

import concourse.mybir as mybir
from concourse.masks import make_identity

K, T, D, V, H, N = 512, 512, 4, 256, 1024, 256
P = 128
PACK = 4
BLOCKS = H // P
HALVES = H // (P * PACK)
SIDES = V // P
FLOPS = 2 * K * H * T + 2 * H * N * V

F32 = mybir.dt.float32
BF16 = mybir.dt.bfloat16
U32 = mybir.dt.uint32
U16 = mybir.dt.uint16
U8 = mybir.dt.uint8
FP8X4 = mybir.dt.float8_e4m3fn_x4
MULT = mybir.AluOpType.mult
RELU = mybir.ActivationFunctionType.Relu
COPY = mybir.ActivationFunctionType.Copy

X_PIECES = ((0, 256), (256, 128), (384, 128))

X_VECTOR_SHARE = 64

W1_PIECES = ((0, 128), (128, 128), (256, 256), (512, 256), (768, 256))

PIECE_BLOCKS = ((0,), (1,), (2, 3), (4, 6), (5, 7))

FUSED = 2

LAST = BLOCKS - 1
SUM_BANKS = ((4, 5), (6, 7), (4, 5), (6, 7), (3, 0), (4, 5), (1, 2), (3, 0))


def tile_picked_gcn_mlp_relu_sub_l_kernel(
    tc, xT, w1, w2, gate, pos1, pos2, pos3, pos4, out
):
    nc = tc.nc
    with ExitStack() as ctx:
        keep = ctx.enter_context(tc.tile_pool(name="keep", bufs=1))
        h_pool = ctx.enter_context(tc.tile_pool(name="h_pool", bufs=BLOCKS))
        psum_one = ctx.enter_context(tc.psum_pool(name="psum_one", bufs=1))


        def load(name, rows):
            raw = keep.tile([P, PACK, rows.shape[1]], F32, name=name)
            nc.sync.dma_start(out=raw[:], in_=rows.rearrange("(p j) w -> p j w", j=PACK))
            return raw

        def load_w1(piece):
            first, count = W1_PIECES[piece]
            return load("w1_raw%d" % piece, w1[:, first : first + count])

        lists = [keep.tile([P, V // 16], U16, name="list%d" % d) for d in range(D)]
        gate01 = keep.tile([P, 2, V], F32, align_bytes=64, name="gate01")
        gate23 = keep.tile([P, 2, V], F32, align_bytes=64, name="gate23")
        gates = [gate01[:, 0, :], gate01[:, 1, :]]

        x_raw = [load("x_raw0", xT[:, 0 : T // 2])[:]]
        w1_raw = [load_w1(0)]
        x_rest = load("x_rest", xT[:, T // 2 : T])
        x_raw.append(x_rest[:, :, 0:P])
        x_raw.append(x_rest[:, :, P : 2 * P])
        w1_raw.append(load_w1(1))
        nc.sync.dma_start(lists[0][:], pos1)
        nc.sync.dma_start(lists[2][:], pos3)
        nc.sync.dma_start(out=gate01[:, 0, :], in_=gate[0])
        nc.sync.dma_start(lists[3][:], pos4)
        w1_raw.append(load_w1(2))
        nc.sync.dma_start(lists[1][:], pos2)
        nc.sync.dma_start(out=gate01[:, 1, :], in_=gate[1])
        nc.sync.dma_start(out=gate23[:], in_=gate[2:4].rearrange("d p v -> p d v"))
        for piece in range(3, len(W1_PIECES)):
            w1_raw.append(load_w1(piece))
        w2_raw = [load("w2_raw%d" % half, w2[P * PACK * half : P * PACK * (half + 1), :]) for half in range(HALVES)]

        identity = keep.tile([P, P], F32, name="identity")
        make_identity(nc, identity[:])


        def interleave(copy, grouped, raw):
            copy(
                out=grouped.rearrange("p (c i) j -> p c j i", i=4),
                in_=raw.rearrange("p j (c i) -> p c j i", i=4),
            )

        def quantise(codes, scales, grouped):
            nc.vector.quantize_mx(out=codes.bitcast(FP8X4), scales=scales, in_=grouped)

        def operand(name, width, codes_name=None):
            codes = keep.tile([P, width], U32, align_bytes=64, name=codes_name or name + "_codes")
            scales = keep.tile([P, width], U8, align_bytes=64, name=name + "_scales")
            return codes, scales

        x_grouped = [
            keep.tile([P, count, PACK], BF16, align_bytes=64, name="x_grouped%d" % i)
            for i, (first, count) in enumerate(X_PIECES)
        ]
        x_codes, x_scales = operand("x", T)

        def copy_x(piece):
            interleave(nc.vector.tensor_copy, x_grouped[piece][:], x_raw[piece])

        def quantise_x(piece):
            first, count = X_PIECES[piece]
            quantise(
                x_codes[:, first : first + count],
                x_scales[:, first : first + count],
                x_grouped[piece][:].rearrange("p w j -> p (w j)"),
            )

        w1_grouped = []
        w1_quantised = {}

        def copy_w1(piece):
            first, count = W1_PIECES[piece]
            grouped = keep.tile([P, count, PACK], BF16, align_bytes=64, name="w1_grouped%d" % piece)
            if first < P * PACK:
                interleave(nc.vector.tensor_copy, grouped[:], w1_raw[piece][:])
            else:
                nc.vector.tensor_copy(
                    out=grouped[:].rearrange("p (u c e) j -> p c j u e", u=2, e=2),
                    in_=w1_raw[piece][:].rearrange("p j (c u e) -> p c j u e", u=2, e=2),
                )
            w1_grouped.append(grouped)

        def quantise_w1(piece):
            count = W1_PIECES[piece][1]
            codes, scales = operand("w1_%d" % piece, count)
            quantise(codes[:], scales[:], w1_grouped[piece][:].rearrange("p w j -> p (w j)"))
            for i, block in enumerate(PIECE_BLOCKS[piece]):
                w1_quantised[block] = (codes, scales, P * i)

        w2_grouped = []

        def copy_w2(half, name, copy):
            grouped = keep.tile([P, N, PACK], BF16, align_bytes=64, name=name)
            interleave(copy, grouped[:], w2_raw[half][:])
            w2_grouped.append(grouped)


        h_tiles = {}
        zero_first = keep.tile([P, 1], F32, align_bytes=64, name="w1_grouped1")
        nc.gpsimd.memset(zero_first[:], 0.0)
        zero_block_0 = keep.tile([P, 1], F32, align_bytes=64, name="w1_grouped2")
        nc.scalar.activation(out=zero_block_0[:], in_=identity[:, 0:1], func=RELU, scale=-1.0, bias=zero_first[:])

        def project(block, first, count, result):
            codes, scales, column = w1_quantised[block]
            nc.tensor.matmul_mx(
                out=result,
                lhsT=codes[:, column : column + P].bitcast(FP8X4),
                lhsT_scale=scales[:, column : column + P],
                rhs=x_codes[:, first : first + count].bitcast(FP8X4),
                rhs_scale=x_scales[:, first : first + count],
                start=True,
                stop=True,
            )

        def first_product_of_block_0(piece):
            if piece == 0:
                h_tiles[0] = h_pool.tile([P, T], F32, name="h")
            h = h_tiles[0]
            first, count = X_PIECES[piece]
            result = psum_one.tile([P, count], F32, name="bank%d" % piece)
            project(0, first, count, result[:])
            if piece == 1:
                nc.vector.tensor_scalar_max(h[:, first : first + count], result[:], zero_block_0[:])
            else:
                nc.scalar.activation(out=h[:, first : first + count], in_=result[:], func=RELU, bias=zero_block_0[:])

        products = [[] for block in range(BLOCKS)]

        def first_product(block):
            if block == 1:
                for first, bank in ((0, "bank3"), (T // 2, "bank0")):
                    result = psum_one.tile([P, T // 2], F32, name=bank)
                    project(block, first, T // 2, result[:])
                    products[block].append((first, T // 2, result))
            else:
                result = psum_one.tile([P, T], F32, name="bank%d" % {2: 1, 3: 2, 4: 3, 6: 0, 5: 1, 7: 2}[block])
                project(block, 0, T, result[:])
                products[block].append((0, T, result))

        def relu(block):
            h = h_pool.tile([P, T], F32, name="h")
            for first, count, result in products[block]:
                nc.scalar.activation(out=h[:, first : first + count], in_=result[:], func=RELU)
            h_tiles[block] = h


        summed0 = keep.tile([P, SIDES, 2, P, 2], BF16, align_bytes=64, name="summed0")
        summed1 = [
            [keep.tile([P, P, 2], BF16, align_bytes=64, name="summed1_%d_%d" % (side, u)) for u in range(2)]
            for side in range(SIDES)
        ]

        def gather(g, block, d, first=0, end=V):
            nc.vector.tensor_tensor(
                g,
                h_tiles[block][:].indirect(lists[d][:, first // 16 : end // 16]),
                gates[d][:, first:end],
                MULT,
            )

        def add_turned(total, g, turn_number):
            nc.tensor.matmul(
                total,
                lhsT=g,
                rhs=identity[:],
                start=(turn_number == 0),
                stop=(turn_number == D - 1),
                is_transpose=True,
            )

        def leave(block, side, total):
            half, quarter = divmod(block, PACK)
            if half == 0:
                nc.scalar.copy(
                    out=summed0[:, side, :, 32 * quarter : 32 * (quarter + 1), :],
                    in_=total.rearrange("v (p u e) -> v u p e", u=2, e=2),
                )
            else:
                u, pair = divmod(quarter, 2)
                nc.scalar.copy(
                    out=summed1[side][u][:, 64 * pair : 64 * (pair + 1), :],
                    in_=total.rearrange("v (p e) -> v p e", e=2),
                )

        def fetch(g, block, d):
            nc.scalar.activation(g, h_tiles[block][:].indirect(lists[d][:]), COPY)

        def sum_banks(block):
            names = ["bank%d" % bank for bank in SUM_BANKS[block]]
            return [psum_one.tile([P, P], F32, name=name) for name in names]


        z0_grouped = keep.tile([P, SIDES, P * PACK], BF16, align_bytes=64, name="z0_grouped")
        z1_grouped = [
            keep.tile([P, P * PACK], BF16, align_bytes=64, name="z1_grouped%d" % side) for side in range(SIDES)
        ]
        z_grouped = [[z0_grouped[:, side, :] for side in range(SIDES)], [z1_grouped[side][:] for side in range(SIDES)]]

        def turn(turned, half, side, u):
            pairs = summed0[:, side, u] if half == 0 else summed1[side][u][:]
            words = pairs.rearrange("v p e -> v (p e)").bitcast(F32)
            nc.tensor.transpose(turned[:, u, :], words, identity[:])

        def turn_back(half, side, bank):
            turned = psum_one.tile([P, 2, P], F32, name=bank)
            for u in range(2):
                turn(turned, half, side, u)
            weave(turned, half, side)

        def weave(turned, half, side):
            nc.scalar.copy(
                out=z_grouped[half][side].bitcast(F32).rearrange("p (c i u) -> p c u i", i=2, u=2),
                in_=turned[:].rearrange("p u (c i) -> p c u i", i=2),
            )


        copy_x(0)
        copy_w1(0)
        quantise_x(0)
        quantise_w1(0)
        copy_x(1)
        interleave(nc.vector.tensor_copy, x_grouped[2][:, 0:X_VECTOR_SHARE, :], x_raw[2][:, :, 0:X_VECTOR_SHARE])
        interleave(nc.scalar.copy, x_grouped[2][:, X_VECTOR_SHARE:P, :], x_raw[2][:, :, X_VECTOR_SHARE:P])
        quantise_x(1)
        quantise_x(2)
        first_product_of_block_0(0)
        copy_w1(1)
        first_product_of_block_0(1)
        first_product_of_block_0(2)
        quantise_w1(1)
        first_product(1)

        sums = []
        turned1 = []
        for block in range(BLOCKS):
            piece = block + 2
            makes_pair = piece < len(W1_PIECES)
            empties_pair = 0 < 2 * block < BLOCKS

            fetched = keep.tile([P, D - FUSED, V], F32, align_bytes=64, name="fetched%d" % block)
            for d in range(FUSED, D):
                fetch(fetched[:, d - FUSED, :], block, d)
            if block > 1:
                for side in range(SIDES):
                    leave(block - 2, side, sums[block - 2][side][:])
            sums.append(sum_banks(block))
            if block == 0:
                relu(1)
            if empties_pair:
                for other in PIECE_BLOCKS[block + 1]:
                    relu(other)
            if block == LAST:
                for side in range(SIDES):
                    leave(block - 1, side, sums[block - 1][side][:])
                turn_back(0, 0, "bank6")
                turn_back(0, 1, "bank7")
                copy_w2(0, "w2_grouped0", nc.scalar.copy)
                w2_left = keep.tile([P, P, PACK], BF16, align_bytes=64, name="fetched5")
                interleave(nc.scalar.copy, w2_left[:], w2_raw[1][:, :, 0:P])

            whole = FUSED if block < LAST else FUSED - 1
            for d in range(whole):
                g = keep.tile([P, V], F32, align_bytes=64, name="g%d_%d" % (block, d))
                gather(g[:], block, d)
                for side in range(SIDES):
                    add_turned(sums[block][side][:], g[:, P * side : P * (side + 1)], d)
                if makes_pair and d == 0:
                    copy_w1(piece)
                if makes_pair and d == 1:
                    quantise_w1(piece)
                    for other in PIECE_BLOCKS[piece]:
                        first_product(other)
            if block == LAST:
                for side, bank in enumerate(("bank4", "bank5")):
                    turned1.append(psum_one.tile([P, 2, P], F32, name=bank))
                    turn(turned1[side], 1, side, 0)
            gated = keep.tile([P, D - FUSED, V], F32, name="gated%d" % block)
            nc.vector.tensor_tensor(gated[:], fetched[:], gate23[:], MULT)
            for j in range(D - FUSED):
                for side in range(SIDES):
                    add_turned(sums[block][side][:], gated[:, j, P * side : P * (side + 1)], whole + j)

        for side in range(SIDES):
            g = keep.tile([P, P], F32, align_bytes=64, name="last_g%d" % side)
            gather(g[:], LAST, 1, P * side, P * (side + 1))
            add_turned(sums[LAST][side][:], g[:], D - 1)
            leave(LAST, side, sums[LAST][side][:])
        for side in range(SIDES):
            turn(turned1[side], 1, side, 1)
            weave(turned1[side], 1, side)

        w2_quantised = [operand("w2_0", N, "last_g1"), operand("w2_1", N)]

        def quantise_w2(half, columns, grouped):
            codes, scales = w2_quantised[half]
            quantise(codes[:, columns], scales[:, columns], grouped[:].rearrange("p w j -> p (w j)"))

        w2_right = keep.tile([P, P, PACK], BF16, align_bytes=64, name="gate01")
        interleave(nc.vector.tensor_copy, w2_right[:], w2_raw[1][:, :, P:N])
        quantise_w2(0, slice(0, N), w2_grouped[0])
        z0_codes, z0_scales = operand("z0", V, "last_g0")
        quantise(z0_codes[:], z0_scales[:], z0_grouped[:].rearrange("p s w -> p (s w)"))
        quantise_w2(1, slice(P, N), w2_right)
        quantise_w2(1, slice(0, P), w2_left)
        z1 = [operand("z1_%d" % side, P) for side in range(SIDES)]
        for side in range(SIDES):
            quantise(z1[side][0][:], z1[side][1][:], z1_grouped[side][:])

        def second_product(result, half, rows, codes, scales, start):
            columns = slice(P * rows, P * (rows + 1))
            w2_codes, w2_scales = w2_quantised[half]
            nc.tensor.matmul_mx(
                out=result,
                lhsT=w2_codes[:, columns].bitcast(FP8X4),
                lhsT_scale=w2_scales[:, columns],
                rhs=codes.bitcast(FP8X4),
                rhs_scale=scales,
                start=start,
                stop=not start,
            )

        banks = [
            [psum_one.tile([P, P], F32, name=name) for name in names]
            for names in (("bank6", "bank7"), ("bank1", "bank2"))
        ]
        for side in range(SIDES):
            targets = slice(P * side, P * (side + 1))
            for rows in range(N // P):
                second_product(banks[side][rows][:], 0, rows, z0_codes[:, targets], z0_scales[:, targets], True)
        for side in range(SIDES):
            for rows in range(N // P):
                second_product(banks[side][rows][:], 1, rows, z1[side][0][:], z1[side][1][:], False)

        copies = (nc.vector.tensor_copy, nc.scalar.copy)
        stored0 = keep.tile([P, N // P, P], F32, name="stored0")
        for rows in range(N // P):
            copies[rows](out=stored0[:, rows, :], in_=banks[0][rows][:])
        nc.sync.dma_start(out=out[:, 0:P].rearrange("(r p) v -> p r v", p=P), in_=stored0[:])
        for rows, queue in enumerate((nc.sync, nc.scalar)):
            stored1 = keep.tile([P, P], F32, name="stored1_%d" % rows)
            copies[rows](out=stored1[:], in_=banks[1][rows][:])
            queue.dma_start(out=out[P * rows : P * (rows + 1), P:V], in_=stored1[:])
